import numpy as np
import ml_dtypes


def mxq(x, axis, fmt="e4m3"):
    dtype, down = {"e4m3": (ml_dtypes.float8_e4m3fn, 7), "e5m2": (ml_dtypes.float8_e5m2, 14)}[fmt]
    v = np.moveaxis(np.asarray(x, np.float32).astype(ml_dtypes.bfloat16).astype(np.float64), axis, -1)
    blocks = v.reshape(v.shape[:-1] + (-1, 32))
    amax = np.abs(blocks).max(-1, keepdims=True)
    byte = np.maximum(np.where(amax > 0, np.frexp(amax)[1] - 1 + 127, 0) - down, 1)
    scale = np.exp2(byte - 127.0)
    codes = (blocks / scale).astype(np.float32).astype(dtype).astype(np.float64)
    return np.moveaxis((codes * scale).reshape(v.shape), -1, axis)


WIDE = False


def mx_kscale(k):
    if not WIDE:
        return np.ones(k)
    levels = np.array([10, -10, 5, -5, 0])
    if k % 512:
        return np.exp2(np.random.permutation(np.resize(levels, k // 32))).repeat(32)
    a = np.empty((k // 512, 16))
    for p in range(k // 512):
        a[p, :8] = np.random.permutation(np.resize(levels, 8))
        for g in range(8):
            far = levels[np.abs(levels - a[p, g]) >= 10]
            a[p, g + 8] = far[np.random.randint(len(far))]
    return np.exp2(a.ravel()).repeat(32)


BF16 = ml_dtypes.bfloat16


def bf(x):
    return np.asarray(x, np.float32).astype(BF16)


def f64(x):
    return np.asarray(x).astype(np.float64)


E2M1 = np.array([0.0, 0.5, 1.0, 1.5, 2.0, 3.0, 4.0, 6.0, -0.0, -0.5, -1.0, -1.5, -2.0, -3.0, -4.0, -6.0])


def pack_weight(w, fmt):
    k, n = w.shape
    w = f64(bf(w)).reshape(k // 32, 32, n)
    amax = np.abs(w).max(1)
    if fmt == "e4m3":
        byte = np.frexp(amax)[1] - 1 + 127 - 7
    else:
        mant, ex = np.frexp(amax / 6.0)
        byte = np.where(mant > 0.5, ex, ex - 1) + 127
    byte = np.clip(np.where(amax > 0, byte, 1), 1, 254)
    scaled = (w * np.exp2(127.0 - byte)[:, None, :]).reshape(k, n).astype(np.float32)
    by_word = np.ascontiguousarray(scaled.reshape(k // 512, 128, 4, n).transpose(0, 1, 3, 2))
    if fmt == "e4m3":
        words = by_word.astype(ml_dtypes.float8_e4m3fn).view(np.uint8)
    else:
        c = by_word.astype(ml_dtypes.float4_e2m1fn).view(np.uint8) & 0xF
        words = c[..., 0::2] | (c[..., 1::2] << 4)
    return np.ascontiguousarray(words), np.ascontiguousarray(byte.astype(np.uint8).reshape(k // 512, 16, n))


def unpack_weight(words, scales, fmt):
    g, p, n, _ = words.shape
    if fmt == "e4m3":
        vals = np.ascontiguousarray(words).view(ml_dtypes.float8_e4m3fn).astype(np.float64)
    else:
        nib = np.empty((g, p, n, 4), np.uint8)
        nib[..., 0::2] = words & 0xF
        nib[..., 1::2] = words >> 4
        vals = E2M1[nib]
    vals = vals * np.repeat(np.exp2(scales.astype(np.float64) - 127.0), 8, axis=1)[..., None]
    return vals.transpose(0, 1, 3, 2).reshape(g * 512, n)
def pack4(w):
    words, scales = pack_weight(w, "e2m1")
    return words.reshape(words.shape[0], 128, -1), scales


def unpack4(words, scales):
    return unpack_weight(words.reshape(words.shape[0], 128, -1, 2), scales, "e2m1")


def planes(Y):
    n, m = Y.shape
    b = f64(bf(Y)).reshape(n // 32, 32, m)
    amax = np.abs(b).max(1)
    byte = np.clip(np.where(amax > 0, np.frexp(amax)[1] - 1 + 127 - 7, 1), 1, 254)
    codes = (b * np.exp2(127.0 - byte)[:, None, :]).reshape(n, m).astype(np.float32).astype(ml_dtypes.float8_e4m3fn).view(np.uint8)
    words = codes.reshape(n // 512, 128, 4, m).transpose(0, 1, 3, 2)
    return np.ascontiguousarray(words), np.ascontiguousarray(byte.astype(np.uint8).reshape(n // 512, 16, m))


M, A, K, F, D, N = 1536, 512, 1024, 1024, 2048, 512
LEVEL = 0.4
SPREAD = 1.8


def setup_inputs():
    rnd = np.random.randn
    s, t = mx_kscale(K), mx_kscale(F)
    x = rnd(M, K) * np.exp(LEVEL * rnd(M, 1)) * s
    wr, wi = rnd(A, F) / np.sqrt(K), rnd(A, F) / np.sqrt(K)
    w = np.concatenate([np.concatenate([wr, wi], 1), np.concatenate([-wi, wr], 1)], 0) / s[:, None]
    x_words, x_scales = pack_weight(x.T, "e4m3")
    w_words, w_scales = pack4(w)
    pool = np.exp(SPREAD * rnd(F, N) - 0.5 * SPREAD ** 2) / F
    return {
        "x_words": x_words, "x_scales": x_scales,
        "w_words": w_words, "w_scales": w_scales,
        "cal": bf(np.exp(0.3 * rnd(F)) * t),
        "pool": bf(pool / t[:, None]),
        "base": bf(0.2 + 0.3 * np.abs(rnd(N))),
        "gamma": bf(np.exp(0.7 * rnd(N))),
        "beta": bf(0.5 * rnd(N)),
    }


def reference(x_words, x_scales, w_words, w_scales, cal, pool, base, gamma, beta):
    X = unpack_weight(x_words, x_scales, "e4m3")
    W = unpack4(w_words, w_scales)
    z = X.T @ W
    re, im = z[:, :F], z[:, F:]
    h = (re * re + im * im) * f64(cal)
    e = mxq(h, 1, "e4m3") @ mxq(f64(pool), 0, "e4m3")
    y = f64(gamma) * np.log(e + f64(base)) + f64(beta)
    Y = y.T
    words, scales = planes(Y)
    return y, words, scales

@@ -1,0 +1,357 @@
+from contextlib import ExitStack
+
+import concourse.mybir as mybir
+from concourse.masks import make_identity
+
+M, K, F, D, N = 1536, 1024, 1024, 2048, 512
+FLOPS = 2 * M * K * D + 2 * M * F * N
+
+F32 = mybir.dt.float32
+BF16 = mybir.dt.bfloat16
+I32 = mybir.dt.int32
+U32 = mybir.dt.uint32
+U8 = mybir.dt.uint8
+FP8X4 = mybir.dt.float8_e4m3fn_x4
+FP4X4 = mybir.dt.float4_e2m1fn_x4
+ACT = mybir.ActivationFunctionType
+ALU = mybir.AluOpType
+
+P = 128
+PACK = 4
+CH = 512
+RE0, RE1, IM0, IM1 = 0, 1, 2, 3
+
+
+def tile_beam_power_log_bands_h2_kernel(
+    tc, x_words, x_scales, w_words, w_scales, cal, pool, base, gamma, beta, out_0, out_1, out_2
+):
+    nc = tc.nc
+    with ExitStack() as ctx:
+        keep = ctx.enter_context(tc.tile_pool(name="keep", bufs=1))
+        work = ctx.enter_context(tc.tile_pool(name="work", bufs=2))
+        psum_mm = ctx.enter_context(tc.psum_pool(name="psum_mm", bufs=4))
+        psum_tr = ctx.enter_context(tc.psum_pool(name="psum_tr", bufs=4))
+        ctx.enter_context(tc.manual_schedule())
+
+        def kept(name, shape, dtype):
+            return keep.tile(shape, dtype, name=name, align_bytes=64)
+
+        ws_first = kept("ws_first", [P, 2, CH], U8)
+        ws_rest = kept("ws_rest", [P, 2, 3 * CH], U8)
+        xs_first = kept("xs_first", [P, 2, CH], U8)
+        xs_rest = kept("xs_rest", [P, 2, 2 * CH], U8)
+        cal_rows = kept("cal_rows", [P, 2 * P], BF16)
+        one = kept("one", [P, 1], F32)
+        warm_sqrt = kept("warm_sqrt", [P, 1], F32)
+        warm_ln = kept("warm_ln", [P, 1], F32)
+        ident_bf = kept("ident_bf", [P, P], BF16)
+        ident_f32 = kept("ident_f32", [P, P], F32)
+        base_col = kept("base_col", [P, PACK], BF16)
+        gamma_col = kept("gamma_col", [P, PACK], BF16)
+        beta_col = kept("beta_col", [P, PACK], BF16)
+        cal_abs = kept("cal_abs", [P, 2, PACK], F32)
+        cal_root = kept("cal_root", [P, 2 * PACK], F32)
+        cal_step = kept("cal_step", [P, 2, PACK], F32)
+        cal_sign = kept("cal_sign", [P, 2, PACK], BF16)
+        w_raw = [kept("w_raw%d" % q, [P, 2, 2 * CH], U8) for q in range(4)]
+        w_codes = [kept("w_codes%d" % q, [P, 2, 2 * CH], U8) for q in range(4)]
+        w_planes = [kept("w_planes%d" % q, [P, 2, CH], U8) for q in range(4)]
+        x_codes = [kept("x_codes%d" % c, [P, 2, CH], U32) for c in range(3)]
+        pool_raw = [kept("pool_raw%d" % g, [P, PACK, N], BF16) for g in range(2)]
+        pool_grouped = [kept("pool_grouped%d" % g, [P, N * PACK], BF16) for g in range(2)]
+        pool_codes = [kept("pool_codes%d" % g, [P, N], U32) for g in range(2)]
+        pool_planes = [kept("pool_planes%d" % g, [P, N], U8) for g in range(2)]
+        y_codes = [kept("y_codes%d" % c, [P, CH], U32) for c in range(3)]
+        y_plane = kept("y_plane", [P, M], U8)
+
+        def zero_plane(plane):
+            nc.vector.memset(plane[:].bitcast(I32), 0)
+
+        def load_scales(plane, scales, col0, col1, rows=range(4)):
+            by_row = scales.rearrange("g (q r) n -> r q g n", r=4)
+            for r in rows:
+                nc.sync.dma_start(
+                    out=plane[r:P:32, :, :].bitcast(I32),
+                    in_=by_row[r][:, :, col0:col1].bitcast(I32),
+                )
+
+        def load_w(q):
+            src = w_words.rearrange("g p b -> p g b")[:, :, 2 * CH * q : 2 * CH * (q + 1)]
+            nc.sync.dma_start(out=w_raw[q][:].bitcast(I32), in_=src.bitcast(I32))
+
+        def load_x(c):
+            src = x_words.rearrange("g p m t -> p g (m t)")[:, :, PACK * CH * c : PACK * CH * (c + 1)]
+            nc.sync.dma_start(out=x_codes[c][:].bitcast(I32), in_=src.bitcast(I32))
+
+        def load_pool(g):
+            by_row = pool.rearrange("(g b t r) n -> g r b t n", g=2, t=PACK, r=8)
+            for r in range(8):
+                nc.sync.dma_start(out=pool_raw[g][r:P:8, :, :], in_=by_row[g][r])
+
+        nc.vector.memset(one[:], 1.0)
+        nc.vector.memset(cal_rows[:], 0.0)
+        zero_plane(ws_first)
+        zero_plane(xs_first)
+        zero_plane(ws_rest)
+        zero_plane(xs_rest)
+        nc.scalar.activation(out=warm_sqrt[:], in_=one[:], func=ACT.Sqrt)
+        make_identity(nc, ident_bf[:])
+        make_identity(nc, ident_f32[:])
+        nc.gpsimd.dma_start(out=base_col[:], in_=base.rearrange("(p t) -> p t", t=PACK))
+        nc.gpsimd.dma_start(out=gamma_col[:], in_=gamma.rearrange("(p t) -> p t", t=PACK))
+        nc.gpsimd.dma_start(out=beta_col[:], in_=beta.rearrange("(p t) -> p t", t=PACK))
+
+        nc.sync.dma_start(
+            out=cal_rows[0:PACK, :].rearrange("t (b r) -> t b r", r=8),
+            in_=cal.rearrange("(b t r) -> t b r", t=PACK, r=8),
+        )
+        load_scales(ws_first, w_scales, 0, CH)
+        load_w(RE0)
+        load_x(0)
+        load_scales(xs_first, x_scales, 0, CH)
+        load_w(IM0)
+        load_scales(ws_rest, w_scales, CH, D)
+        load_w(RE1)
+        load_pool(0)
+        load_w(IM1)
+        load_pool(1)
+        load_scales(xs_rest, x_scales, CH, M)
+        load_x(1)
+        load_x(2)
+
+        def order_w(q):
+            raw_plane = ws_first[:] if q == 0 else ws_rest[:, :, CH * (q - 1) : CH * q]
+            nc.vector.tensor_copy(
+                out=w_planes[q][:].bitcast(I32).rearrange("p g (t b w) -> p g t b w", t=PACK, w=2),
+                in_=raw_plane.bitcast(I32).rearrange("p g (b t w) -> p g t b w", t=PACK, w=2),
+            )
+            nc.vector.tensor_copy(
+                out=w_codes[q][:].bitcast(I32).rearrange("p g (t b w) -> p g t b w", t=PACK, w=4),
+                in_=w_raw[q][:].bitcast(I32).rearrange("p g (b t w) -> p g t b w", t=PACK, w=4),
+            )
+
+        def x_plane(c, g):
+            return xs_first[:, g, :] if c == 0 else xs_rest[:, g, CH * (c - 1) : CH * c]
+
+        squares = {}
+
+        def beam(c, j):
+            g, part, t = j // 8, (j // 4) % 2, j % 4
+            q = 2 * part + g
+            if t == 0:
+                squares[(c, g, part)] = work.tile(
+                    [P, PACK, CH], F32, name="sq%d" % part, tag="sq%d" % part, bufs=3, align_bytes=64
+                )
+            z = psum_mm.tile([P, CH], F32, name="mm", tag="mm")
+            for kp in range(2):
+                nc.tensor.matmul_mx(
+                    out=z[:],
+                    lhsT=w_codes[q][:, kp, 2 * P * t : 2 * P * (t + 1)].bitcast(FP4X4),
+                    lhsT_scale=w_planes[q][:, kp, P * t : P * (t + 1)],
+                    rhs=x_codes[c][:, kp, :].bitcast(FP8X4),
+                    rhs_scale=x_plane(c, kp),
+                    start=(kp == 0),
+                    stop=(kp == 1),
+                )
+            col = PACK * g + t
+            nc.scalar.activation(
+                out=squares[(c, g, part)][:, t, :], in_=z[:], func=ACT.Square, scale=cal_root[:, col : col + 1]
+            )
+
+        h_bf, h_codes, h_planes = {}, {}, {}
+
+        def power(c, g, m0=0, m1=CH):
+            if m0 == 0:
+                h_bf[(c, g)] = work.tile([P, CH * PACK], BF16, name="h_bf", tag="h_bf", bufs=2, align_bytes=64)
+            nc.vector.tensor_tensor(
+                out=h_bf[(c, g)][:, PACK * m0 : PACK * m1].rearrange("p (c i t) -> p c t i", i=4, t=PACK),
+                in0=squares[(c, g, 0)][:, :, m0:m1].rearrange("p t (c i) -> p c t i", i=4),
+                in1=squares[(c, g, 1)][:, :, m0:m1].rearrange("p t (c i) -> p c t i", i=4),
+                op=ALU.add,
+            )
+
+        def quantize_h(c, g, m0=0, m1=CH):
+            if m0 == 0:
+                h_codes[(c, g)] = work.tile([P, CH], U32, name="h_codes", tag="h_codes", bufs=4, align_bytes=64)
+                h_planes[(c, g)] = work.tile([P, CH], U8, name="h_plane", tag="h_plane", bufs=4, align_bytes=64)
+            nc.vector.quantize_mx(
+                out=h_codes[(c, g)][:, m0:m1].bitcast(FP8X4),
+                scales=h_planes[(c, g)][:, m0:m1],
+                in_=h_bf[(c, g)][:, PACK * m0 : PACK * m1],
+            )
+
+        def group_pool(g):
+            nc.vector.tensor_tensor(
+                out=pool_grouped[g][:].rearrange("p (u m t) -> p m u t", u=PACK, t=PACK),
+                in0=pool_raw[g][:].rearrange("p t (m u) -> p m u t", u=PACK),
+                in1=cal_sign[:, g, :].unsqueeze(1).unsqueeze(1).to_broadcast([P, P, PACK, PACK]),
+                op=ALU.mult,
+            )
+
+        def quantize_pool(g):
+            nc.vector.quantize_mx(
+                out=pool_codes[g][:].bitcast(FP8X4), scales=pool_planes[g][:], in_=pool_grouped[g][:]
+            )
+
+        logs, ys, y_bf = {}, {}, {}
+
+        def bands(c, u, m0=0, m1=CH):
+            if u == 0 and m0 == 0:
+                logs[c] = work.tile([P, PACK, CH], F32, name="logs", tag="logs", bufs=2, align_bytes=64)
+            e = psum_mm.tile([P, m1 - m0], F32, name="mm", tag="mm")
+            for g in range(2):
+                nc.tensor.matmul_mx(
+                    out=e[:],
+                    lhsT=pool_codes[g][:, P * u : P * (u + 1)].bitcast(FP8X4),
+                    lhsT_scale=pool_planes[g][:, P * u : P * (u + 1)],
+                    rhs=h_codes[(c, g)][:, m0:m1].bitcast(FP8X4),
+                    rhs_scale=h_planes[(c, g)][:, m0:m1],
+                    start=(g == 0),
+                    stop=(g == 1),
+                )
+            nc.scalar.activation(out=logs[c][:, u, m0:m1], in_=e[:], func=ACT.Ln, bias=base_col[:, u : u + 1])
+
+        def affine(c, m0=0, m1=CH):
+            if m0 == 0:
+                ys[c] = work.tile([P, PACK, CH], F32, name="ys", tag="ys", bufs=2, align_bytes=64)
+            for u in range(PACK):
+                nc.vector.tensor_scalar(
+                    out=ys[c][:, u, m0:m1],
+                    in0=logs[c][:, u, m0:m1],
+                    scalar1=gamma_col[:, u : u + 1],
+                    scalar2=beta_col[:, u : u + 1],
+                    op0=ALU.mult,
+                    op1=ALU.add,
+                )
+
+        def group_y(c, m0=0, m1=CH):
+            if m0 == 0:
+                y_bf[c] = work.tile([P, CH * PACK], BF16, name="y_bf", tag="y_bf", bufs=2, align_bytes=64)
+            nc.vector.tensor_copy(
+                out=y_bf[c][:, PACK * m0 : PACK * m1].rearrange("p (c i u) -> p c u i", i=4, u=PACK),
+                in_=ys[c][:, :, m0:m1].rearrange("p u (c i) -> p c u i", i=4),
+            )
+
+        def quantize_y(c, m0=0, m1=CH):
+            nc.vector.quantize_mx(
+                out=y_codes[c][:, m0:m1].bitcast(FP8X4),
+                scales=y_plane[:, CH * c + m0 : CH * c + m1],
+                in_=y_bf[c][:, PACK * m0 : PACK * m1],
+            )
+            dst = out_1[0].rearrange("p m t -> p (m t)")[:, PACK * (CH * c + m0) : PACK * (CH * c + m1)]
+            nc.sync.dma_start(out=dst.bitcast(I32), in_=y_codes[c][:, m0:m1].bitcast(I32))
+
+        turned = {}
+
+        def turn(c, m0=0, m1=CH):
+            for row0 in range(m0, m1, P):
+                bank = psum_tr.tile([P, PACK, P], F32, name="tr", tag="tr")
+                turned[(c, row0)] = bank
+                for u in range(PACK):
+                    nc.tensor.transpose(bank[:, u, :], ys[c][:, u, row0 : row0 + P], ident_f32[:])
+
+        def store_rows(c, row0, on_scalar):
+            rows = work.tile([P, N], F32, name="rows", tag="rows", bufs=6, align_bytes=64)
+            dst = rows[:].rearrange("m (p u) -> m p u", u=PACK)
+            src = turned[(c, row0)][:].rearrange("m u p -> m p u")
+            if on_scalar:
+                nc.scalar.copy(out=dst, in_=src)
+            else:
+                nc.vector.tensor_copy(out=dst, in_=src)
+            nc.sync.dma_start(out=out_0[CH * c + row0 : CH * c + row0 + P, :], in_=rows[:])
+
+        cal_t = psum_tr.tile([P, 2, P], BF16, name="tr", tag="tr")
+        for g in range(2):
+            nc.tensor.transpose(cal_t[:, g, :], cal_rows[:, P * g : P * (g + 1)], ident_bf[:])
+        nc.scalar.activation(out=cal_abs[:], in_=cal_t[:, :, 0:PACK], func=ACT.Abs)
+        nc.scalar.activation(out=cal_root[:], in_=cal_abs[:].rearrange("p g t -> p (g t)"), func=ACT.Sqrt)
+        nc.scalar.activation(out=warm_ln[:], in_=one[:], func=ACT.Ln)
+
+        order_w(RE0)
+        nc.vector.tensor_scalar(
+            out=cal_step[:], in0=cal_t[:, :, 0:PACK], scalar1=0.0, scalar2=2.0, op0=ALU.is_ge, op1=ALU.mult
+        )
+        for j in range(4):
+            beam(0, j)
+        order_w(IM0)
+        nc.vector.tensor_scalar(
+            out=cal_sign[:], in0=cal_step[:], scalar1=1.0, scalar2=None, op0=ALU.subtract
+        )
+        order_w(RE1)
+        for j in range(4, 12):
+            beam(0, j)
+        group_pool(0)
+        order_w(IM1)
+        for j in range(12, 16):
+            beam(0, j)
+        quantize_pool(0)
+        power(0, 0)
+        group_pool(1)
+        quantize_h(0, 0)
+        power(0, 1)
+        quantize_pool(1)
+        quantize_h(0, 1)
+
+        for j in range(11):
+            beam(1, j)
+        power(1, 0)
+        bands(0, 0)
+        bands(0, 1)
+        beam(1, 11)
+        bands(0, 2)
+        beam(1, 12)
+        bands(0, 3)
+        for j in range(13, 16):
+            beam(1, j)
+        affine(0)
+        quantize_h(1, 0)
+        turn(0)
+        group_y(0)
+        power(1, 1)
+        quantize_y(0)
+        quantize_h(1, 1)
+        for row0 in range(0, CH, P):
+            store_rows(0, row0, False)
+
+        for j in range(7):
+            beam(2, j)
+        for u in range(PACK):
+            bands(1, u)
+            beam(2, 7 + u)
+        power(2, 0)
+        for j in range(11, 16):
+            beam(2, j)
+        affine(1)
+        quantize_h(2, 0)
+        group_y(1)
+        turn(1)
+
+        half = CH // 2
+        power(2, 1, 0, half)
+        quantize_y(1)
+        quantize_h(2, 1, 0, half)
+        power(2, 1, half, CH)
+        quantize_h(2, 1, half, CH)
+        for row0 in range(0, CH, P):
+            store_rows(1, row0, True)
+        for u in range(PACK):
+            bands(2, u, 0, half)
+        for u in range(PACK):
+            bands(2, u, half, CH)
+        affine(2, 0, half)
+        turn(2, 0, half)
+        group_y(2, 0, half)
+        affine(2, half, CH)
+        turn(2, half, CH)
+        store_rows(2, 0, True)
+        store_rows(2, P, True)
+        quantize_y(2, 0, half)
+        group_y(2, half, CH)
+        store_rows(2, 2 * P, True)
+        quantize_y(2, half, CH)
+        store_rows(2, 3 * P, True)
+        for quad in range(4):
+            nc.sync.dma_start(
+                out=out_2[0][4 * quad : 4 * quad + 4, :].bitcast(I32),
+                in_=y_plane[32 * quad : 32 * quad + 4, :].bitcast(I32),
+            )

@@ -36,14 +36,17 @@ def tile_beam_power_log_bands_h2_kernel(
         def kept(name, shape, dtype):
             return keep.tile(shape, dtype, name=name, align_bytes=64)
 
-        ws_first = kept("ws_first", [P, 2, CH], U8)
-        ws_rest = kept("ws_rest", [P, 2, 3 * CH], U8)
+        ws_first = kept("ws_first", [P, 2, F], U8)
+        ws_rest = kept("ws_rest", [P, 2, F], U8)
         xs_first = kept("xs_first", [P, 2, CH], U8)
         xs_rest = kept("xs_rest", [P, 2, 2 * CH], U8)
         cal_rows = kept("cal_rows", [P, 2 * P], BF16)
         one = kept("one", [P, 1], F32)
         warm_sqrt = kept("warm_sqrt", [P, 1], F32)
         warm_ln = kept("warm_ln", [P, 1], F32)
+        warm_bf = kept("warm_bf", [P, PACK * P], BF16)
+        warm_codes = kept("warm_codes", [P, P], U32)
+        warm_plane = kept("warm_plane", [P, P], U8)
         ident_bf = kept("ident_bf", [P, P], BF16)
         ident_f32 = kept("ident_f32", [P, P], F32)
         base_col = kept("base_col", [P, PACK], BF16)
@@ -84,43 +87,45 @@ def tile_beam_power_log_bands_h2_kernel(
             nc.sync.dma_start(out=x_codes[c][:].bitcast(I32), in_=src.bitcast(I32))
 
         def load_pool(g):
-            by_row = pool.rearrange("(g b t r) n -> g r b t n", g=2, t=PACK, r=8)
-            for r in range(8):
-                nc.sync.dma_start(out=pool_raw[g][r:P:8, :, :], in_=by_row[g][r])
+            by_slot = pool.rearrange("(g b t r) n -> g t b r n", g=2, t=PACK, r=8)
+            for t in range(PACK):
+                nc.sync.dma_start(out=pool_raw[g][:, t, :], in_=by_slot[g][t])
 
-        nc.vector.memset(one[:], 1.0)
         nc.vector.memset(cal_rows[:], 0.0)
+        nc.vector.memset(one[:], 1.0)
         zero_plane(ws_first)
         zero_plane(xs_first)
-        zero_plane(ws_rest)
-        zero_plane(xs_rest)
         nc.scalar.activation(out=warm_sqrt[:], in_=one[:], func=ACT.Sqrt)
         make_identity(nc, ident_bf[:])
         make_identity(nc, ident_f32[:])
-        nc.gpsimd.dma_start(out=base_col[:], in_=base.rearrange("(p t) -> p t", t=PACK))
-        nc.gpsimd.dma_start(out=gamma_col[:], in_=gamma.rearrange("(p t) -> p t", t=PACK))
-        nc.gpsimd.dma_start(out=beta_col[:], in_=beta.rearrange("(p t) -> p t", t=PACK))
+        nc.vector.memset(warm_bf[:], 1.0)
+        nc.vector.quantize_mx(out=warm_codes[:].bitcast(FP8X4), scales=warm_plane[:], in_=warm_bf[:])
 
         nc.sync.dma_start(
             out=cal_rows[0:PACK, :].rearrange("t (b r) -> t b r", r=8),
             in_=cal.rearrange("(b t r) -> t b r", t=PACK, r=8),
         )
-        load_scales(ws_first, w_scales, 0, CH)
         load_w(RE0)
+        load_scales(ws_first, w_scales, 0, F)
+        zero_plane(ws_rest)
+        zero_plane(xs_rest)
         load_x(0)
         load_scales(xs_first, x_scales, 0, CH)
-        load_w(IM0)
-        load_scales(ws_rest, w_scales, CH, D)
         load_w(RE1)
+        load_scales(ws_rest, w_scales, F, D)
+        load_w(IM0)
         load_pool(0)
         load_w(IM1)
         load_pool(1)
         load_scales(xs_rest, x_scales, CH, M)
         load_x(1)
+        nc.sync.dma_start(out=base_col[:], in_=base.rearrange("(p t) -> p t", t=PACK))
+        nc.sync.dma_start(out=gamma_col[:], in_=gamma.rearrange("(p t) -> p t", t=PACK))
+        nc.sync.dma_start(out=beta_col[:], in_=beta.rearrange("(p t) -> p t", t=PACK))
         load_x(2)
 
         def order_w(q):
-            raw_plane = ws_first[:] if q == 0 else ws_rest[:, :, CH * (q - 1) : CH * q]
+            raw_plane = (ws_first, ws_rest)[q // 2][:, :, CH * (q % 2) : CH * (q % 2 + 1)]
             nc.vector.tensor_copy(
                 out=w_planes[q][:].bitcast(I32).rearrange("p g (t b w) -> p g t b w", t=PACK, w=2),
                 in_=raw_plane.bitcast(I32).rearrange("p g (b t w) -> p g t b w", t=PACK, w=2),
@@ -135,7 +140,7 @@ def tile_beam_power_log_bands_h2_kernel(
 
         squares = {}
 
-        def beam(c, j):
+        def beam(c, j, cuts=((0, CH),)):
             g, part, t = j // 8, (j // 4) % 2, j % 4
             q = 2 * part + g
             if t == 0:
@@ -154,9 +159,13 @@ def tile_beam_power_log_bands_h2_kernel(
                     stop=(kp == 1),
                 )
             col = PACK * g + t
-            nc.scalar.activation(
-                out=squares[(c, g, part)][:, t, :], in_=z[:], func=ACT.Square, scale=cal_root[:, col : col + 1]
-            )
+            for m0, m1 in cuts:
+                nc.scalar.activation(
+                    out=squares[(c, g, part)][:, t, m0:m1],
+                    in_=z[:, m0:m1],
+                    func=ACT.Square,
+                    scale=cal_root[:, col : col + 1],
+                )
 
         h_bf, h_codes, h_planes = {}, {}, {}
 
@@ -181,12 +190,20 @@ def tile_beam_power_log_bands_h2_kernel(
             )
 
         def group_pool(g):
-            nc.vector.tensor_tensor(
+            nc.vector.tensor_copy(
                 out=pool_grouped[g][:].rearrange("p (u m t) -> p m u t", u=PACK, t=PACK),
-                in0=pool_raw[g][:].rearrange("p t (m u) -> p m u t", u=PACK),
-                in1=cal_sign[:, g, :].unsqueeze(1).unsqueeze(1).to_broadcast([P, P, PACK, PACK]),
-                op=ALU.mult,
+                in_=pool_raw[g][:].rearrange("p t (m u) -> p m u t", u=PACK),
             )
+
+        def sign_pool(g):
+            for t in range(PACK):
+                nc.vector.tensor_scalar(
+                    out=pool_raw[g][:, t, :],
+                    in0=pool_raw[g][:, t, :],
+                    scalar1=cal_sign[:, g, t : t + 1],
+                    scalar2=None,
+                    op0=ALU.mult,
+                )
 
         def quantize_pool(g):
             nc.vector.quantize_mx(
@@ -211,10 +228,10 @@ def tile_beam_power_log_bands_h2_kernel(
                 )
             nc.scalar.activation(out=logs[c][:, u, m0:m1], in_=e[:], func=ACT.Ln, bias=base_col[:, u : u + 1])
 
-        def affine(c, m0=0, m1=CH):
-            if m0 == 0:
+        def affine(c, m0=0, m1=CH, slots=range(PACK)):
+            if m0 == 0 and 0 in slots:
                 ys[c] = work.tile([P, PACK, CH], F32, name="ys", tag="ys", bufs=2, align_bytes=64)
-            for u in range(PACK):
+            for u in slots:
                 nc.vector.tensor_scalar(
                     out=ys[c][:, u, m0:m1],
                     in0=logs[c][:, u, m0:m1],
@@ -260,9 +277,24 @@ def tile_beam_power_log_bands_h2_kernel(
                 nc.vector.tensor_copy(out=dst, in_=src)
             nc.sync.dma_start(out=out_0[CH * c + row0 : CH * c + row0 + P, :], in_=rows[:])
 
+        def warm_tensor(passes):
+            idle = psum_mm.tile([P, P], F32, name="mm", tag="mm")
+            for i in range(passes):
+                nc.tensor.matmul_mx(
+                    out=idle[:],
+                    lhsT=warm_codes[:].bitcast(FP8X4),
+                    lhsT_scale=warm_plane[:],
+                    rhs=warm_codes[:].bitcast(FP8X4),
+                    rhs_scale=warm_plane[:],
+                    start=True,
+                    stop=True,
+                )
+
+        warm_tensor(4)
         cal_t = psum_tr.tile([P, 2, P], BF16, name="tr", tag="tr")
         for g in range(2):
             nc.tensor.transpose(cal_t[:, g, :], cal_rows[:, P * g : P * (g + 1)], ident_bf[:])
+        warm_tensor(14)
         nc.scalar.activation(out=cal_abs[:], in_=cal_t[:, :, 0:PACK], func=ACT.Abs)
         nc.scalar.activation(out=cal_root[:], in_=cal_abs[:].rearrange("p g t -> p (g t)"), func=ACT.Sqrt)
         nc.scalar.activation(out=warm_ln[:], in_=one[:], func=ACT.Ln)
@@ -273,85 +305,108 @@ def tile_beam_power_log_bands_h2_kernel(
         )
         for j in range(4):
             beam(0, j)
-        order_w(IM0)
+        order_w(RE1)
         nc.vector.tensor_scalar(
             out=cal_sign[:], in0=cal_step[:], scalar1=1.0, scalar2=None, op0=ALU.subtract
         )
-        order_w(RE1)
-        for j in range(4, 12):
+        order_w(IM0)
+        for j in (8, 9, 10, 11, 4, 5, 6, 7):
             beam(0, j)
-        group_pool(0)
+        sign_pool(0)
         order_w(IM1)
         for j in range(12, 16):
             beam(0, j)
+        group_pool(0)
+        sign_pool(1)
         quantize_pool(0)
-        power(0, 0)
         group_pool(1)
-        quantize_h(0, 0)
-        power(0, 1)
+        power(0, 0)
         quantize_pool(1)
+        power(0, 1)
+        quantize_h(0, 0)
         quantize_h(0, 1)
 
-        for j in range(11):
+        for j in range(10):
             beam(1, j)
         power(1, 0)
-        bands(0, 0)
-        bands(0, 1)
-        beam(1, 11)
-        bands(0, 2)
-        beam(1, 12)
-        bands(0, 3)
-        for j in range(13, 16):
+        for u in range(PACK):
+            bands(0, u)
+            beam(1, 10 + u)
+        for j in range(10 + 4, 16):
             beam(1, j)
-        affine(0)
+        affine(0, slots=(0, 1))
         quantize_h(1, 0)
+        affine(0, slots=(2, 3))
         turn(0)
+        store_rows(0, 0, True)
         group_y(0)
         power(1, 1)
         quantize_y(0)
         quantize_h(1, 1)
-        for row0 in range(0, CH, P):
+        for row0 in range(P, CH, P):
             store_rows(0, row0, False)
 
-        for j in range(7):
+        for j in range(8):
             beam(2, j)
         for u in range(PACK):
             bands(1, u)
-            beam(2, 7 + u)
+            beam(2, 8 + u)
         power(2, 0)
-        for j in range(11, 16):
+        for j in range(8 + 4, 15):
             beam(2, j)
-        affine(1)
+        beam(2, 15, ((0, P), (P, CH)))
+        affine(1, slots=(0, 1))
         quantize_h(2, 0)
+        affine(1, slots=(2, 3))
         group_y(1)
         turn(1)
-
-        half = CH // 2
-        power(2, 1, 0, half)
         quantize_y(1)
-        quantize_h(2, 1, 0, half)
-        power(2, 1, half, CH)
-        quantize_h(2, 1, half, CH)
-        for row0 in range(0, CH, P):
-            store_rows(1, row0, True)
-        for u in range(PACK):
-            bands(2, u, 0, half)
-        for u in range(PACK):
-            bands(2, u, half, CH)
-        affine(2, 0, half)
-        turn(2, 0, half)
-        group_y(2, 0, half)
-        affine(2, half, CH)
-        turn(2, half, CH)
+        store_rows(1, 0, True)
+        store_rows(1, 128, True)
+        store_rows(1, 256, True)
+        store_rows(1, 384, True)
+        power(2, 1, 0, 128)
+        power(2, 1, 128, 256)
+        quantize_h(2, 1, 0, 128)
+        power(2, 1, 256, 384)
+        quantize_h(2, 1, 128, 256)
+        power(2, 1, 384, 512)
+        quantize_h(2, 1, 256, 384)
+        bands(2, 0, 0, 128)
+        bands(2, 1, 0, 128)
+        bands(2, 2, 0, 128)
+        bands(2, 3, 0, 128)
+        bands(2, 0, 128, 256)
+        bands(2, 1, 128, 256)
+        bands(2, 2, 128, 256)
+        bands(2, 3, 128, 256)
+        affine(2, 0, 128)
+        quantize_h(2, 1, 384, 512)
+        bands(2, 0, 256, 384)
+        bands(2, 1, 256, 384)
+        bands(2, 2, 256, 384)
+        bands(2, 3, 256, 384)
+        bands(2, 0, 384, 512)
+        bands(2, 1, 384, 512)
+        bands(2, 2, 384, 512)
+        bands(2, 3, 384, 512)
+        turn(2, 0, 128)
+        affine(2, 128, 256)
+        turn(2, 128, 256)
+        group_y(2, 0, 256)
+        affine(2, 256, 384)
+        turn(2, 256, 384)
+        quantize_y(2, 0, 256)
+        affine(2, 384, 512)
+        turn(2, 384, 512)
         store_rows(2, 0, True)
-        store_rows(2, P, True)
-        quantize_y(2, 0, half)
-        group_y(2, half, CH)
-        store_rows(2, 2 * P, True)
-        quantize_y(2, half, CH)
-        store_rows(2, 3 * P, True)
+        store_rows(2, 128, True)
+        group_y(2, 256, 512)
+        store_rows(2, 256, True)
+        quantize_y(2, 256, 512)
         for quad in range(4):
             nc.sync.dma_start(
-                out=out_2[0][4 * quad : 4 * quad + 4, :].bitcast(I32),
-                in_=y_plane[32 * quad : 32 * quad + 4, :].bitcast(I32),
+                out=out_2[0][4 * quad : 4 * quad + 4, 0:1536].bitcast(I32),
+                in_=y_plane[32 * quad : 32 * quad + 4, 0:1536].bitcast(I32),
             )
+        store_rows(2, 384, True)

@@ -91,14 +91,14 @@ def tile_beam_power_log_bands_h2_kernel(
             for t in range(PACK):
                 nc.sync.dma_start(out=pool_raw[g][:, t, :], in_=by_slot[g][t])
 
-        nc.vector.memset(cal_rows[:], 0.0)
+        nc.gpsimd.memset(cal_rows[:].bitcast(I32), 0)
+        nc.gpsimd.memset(ws_first[:].bitcast(I32), 0)
         nc.vector.memset(one[:], 1.0)
-        zero_plane(ws_first)
+        nc.vector.memset(warm_bf[:], 1.0)
         zero_plane(xs_first)
         nc.scalar.activation(out=warm_sqrt[:], in_=one[:], func=ACT.Sqrt)
         make_identity(nc, ident_bf[:])
         make_identity(nc, ident_f32[:])
-        nc.vector.memset(warm_bf[:], 1.0)
         nc.vector.quantize_mx(out=warm_codes[:].bitcast(FP8X4), scales=warm_plane[:], in_=warm_bf[:])
 
         nc.sync.dma_start(
@@ -255,6 +255,8 @@ def tile_beam_power_log_bands_h2_kernel(
                 scales=y_plane[:, CH * c + m0 : CH * c + m1],
                 in_=y_bf[c][:, PACK * m0 : PACK * m1],
             )
+
+        def store_codes(c, m0=0, m1=CH):
             dst = out_1[0].rearrange("p m t -> p (m t)")[:, PACK * (CH * c + m0) : PACK * (CH * c + m1)]
             nc.sync.dma_start(out=dst.bitcast(I32), in_=y_codes[c][:, m0:m1].bitcast(I32))
 
@@ -267,15 +269,30 @@ def tile_beam_power_log_bands_h2_kernel(
                 for u in range(PACK):
                     nc.tensor.transpose(bank[:, u, :], ys[c][:, u, row0 : row0 + P], ident_f32[:])
 
-        def store_rows(c, row0, on_scalar):
-            rows = work.tile([P, N], F32, name="rows", tag="rows", bufs=6, align_bytes=64)
-            dst = rows[:].rearrange("m (p u) -> m p u", u=PACK)
-            src = turned[(c, row0)][:].rearrange("m u p -> m p u")
-            if on_scalar:
-                nc.scalar.copy(out=dst, in_=src)
-            else:
-                nc.vector.tensor_copy(out=dst, in_=src)
-            nc.sync.dma_start(out=out_0[CH * c + row0 : CH * c + row0 + P, :], in_=rows[:])
+        def store_rows(c, row0, on_scalar, queue=nc.sync, tiles=1):
+            rows = work.tile([P, tiles, N], F32, name="rows", tag="rows", bufs=6, align_bytes=64)
+            for i in range(tiles):
+                dst = rows[:, i, :].rearrange("m (p u) -> m p u", u=PACK)
+                src = turned[(c, row0 + P * i)][:].rearrange("m u p -> m p u")
+                if on_scalar:
+                    nc.scalar.copy(out=dst, in_=src)
+                else:
+                    nc.vector.tensor_copy(out=dst, in_=src)
+            first = CH * c + row0
+            queue.dma_start(out=out_0[first : first + P * tiles, :].rearrange("(i m) n -> m i n", m=P), in_=rows[:])
+
+        def keep_warm(passes):
+            idle = psum_mm.tile([P, CH], F32, name="mm", tag="mm")
+            for i in range(passes):
+                nc.tensor.matmul_mx(
+                    out=idle[:],
+                    lhsT=warm_codes[:].bitcast(FP8X4),
+                    lhsT_scale=warm_plane[:],
+                    rhs=x_codes[0][:, 0, :].bitcast(FP8X4),
+                    rhs_scale=x_plane(0, 0),
+                    start=True,
+                    stop=True,
+                )
 
         def warm_tensor(passes):
             idle = psum_mm.tile([P, P], F32, name="mm", tag="mm")
@@ -290,11 +307,11 @@ def tile_beam_power_log_bands_h2_kernel(
                     stop=True,
                 )
 
-        warm_tensor(4)
+        warm_tensor(8)
         cal_t = psum_tr.tile([P, 2, P], BF16, name="tr", tag="tr")
         for g in range(2):
             nc.tensor.transpose(cal_t[:, g, :], cal_rows[:, P * g : P * (g + 1)], ident_bf[:])
-        warm_tensor(14)
+        warm_tensor(8)
         nc.scalar.activation(out=cal_abs[:], in_=cal_t[:, :, 0:PACK], func=ACT.Abs)
         nc.scalar.activation(out=cal_root[:], in_=cal_abs[:].rearrange("p g t -> p (g t)"), func=ACT.Sqrt)
         nc.scalar.activation(out=warm_ln[:], in_=one[:], func=ACT.Ln)
@@ -337,31 +354,45 @@ def tile_beam_power_log_bands_h2_kernel(
         affine(0, slots=(0, 1))
         quantize_h(1, 0)
         affine(0, slots=(2, 3))
-        turn(0)
+        turn(0, 0, 2 * P)
         store_rows(0, 0, True)
         group_y(0)
         power(1, 1)
         quantize_y(0)
+        store_codes(0)
         quantize_h(1, 1)
-        for row0 in range(P, CH, P):
-            store_rows(0, row0, False)
+        store_rows(0, P, False)
 
-        for j in range(8):
+        for j in range(3):
+            beam(2, j)
+        turn(0, 2 * P, CH)
+        store_rows(0, 2 * P, False)
+        store_rows(0, 3 * P, False)
+        for j in range(3, 8):
             beam(2, j)
         for u in range(PACK):
             bands(1, u)
             beam(2, 8 + u)
         power(2, 0)
-        for j in range(8 + 4, 15):
+        for j in range(8 + 4, 14):
             beam(2, j)
-        beam(2, 15, ((0, P), (P, CH)))
         affine(1, slots=(0, 1))
         quantize_h(2, 0)
         affine(1, slots=(2, 3))
-        group_y(1)
-        turn(1)
-        quantize_y(1)
+        turn(1, 0, 2 * P)
         store_rows(1, 0, True)
+        beam(2, 14)
+        beam(2, 15, ((0, P), (P, CH)))
+        group_y(1)
+        turn(1, 2 * P, CH)
+        keep_warm(2)
+        quantize_y(1)
+        store_codes(1)
+        for quad in range(4):
+            nc.sync.dma_start(
+                out=out_2[0][4 * quad : 4 * quad + 4, 0:1024].bitcast(I32),
+                in_=y_plane[32 * quad : 32 * quad + 4, 0:1024].bitcast(I32),
+            )
         store_rows(1, 128, True)
         store_rows(1, 256, True)
         store_rows(1, 384, True)
@@ -397,16 +428,18 @@ def tile_beam_power_log_bands_h2_kernel(
         affine(2, 256, 384)
         turn(2, 256, 384)
         quantize_y(2, 0, 256)
+        store_codes(2, 0, 256)
         affine(2, 384, 512)
         turn(2, 384, 512)
         store_rows(2, 0, True)
         store_rows(2, 128, True)
         group_y(2, 256, 512)
         store_rows(2, 256, True)
+        store_rows(2, 384, True, nc.scalar)
         quantize_y(2, 256, 512)
+        store_codes(2, 256, 512)
         for quad in range(4):
             nc.sync.dma_start(
-                out=out_2[0][4 * quad : 4 * quad + 4, 0:1536].bitcast(I32),
-                in_=y_plane[32 * quad : 32 * quad + 4, 0:1536].bitcast(I32),
+                out=out_2[0][4 * quad : 4 * quad + 4, 1024:1536].bitcast(I32),
+                in_=y_plane[32 * quad : 32 * quad + 4, 1024:1536].bitcast(I32),
             )
-        store_rows(2, 384, True)

@@ -78,13 +78,13 @@ def tile_beam_power_log_bands_h2_kernel(
                     in_=by_row[r][:, :, col0:col1].bitcast(I32),
                 )
 
-        def load_w(q):
-            src = w_words.rearrange("g p b -> p g b")[:, :, 2 * CH * q : 2 * CH * (q + 1)]
-            nc.sync.dma_start(out=w_raw[q][:].bitcast(I32), in_=src.bitcast(I32))
+        def load_w(q, kps=slice(0, 2)):
+            src = w_words.rearrange("g p b -> p g b")[:, kps, 2 * CH * q : 2 * CH * (q + 1)]
+            nc.sync.dma_start(out=w_raw[q][:, kps, :].bitcast(I32), in_=src.bitcast(I32))
 
-        def load_x(c):
-            src = x_words.rearrange("g p m t -> p g (m t)")[:, :, PACK * CH * c : PACK * CH * (c + 1)]
-            nc.sync.dma_start(out=x_codes[c][:].bitcast(I32), in_=src.bitcast(I32))
+        def load_x(c, kps=slice(0, 2)):
+            src = x_words.rearrange("g p m t -> p g (m t)")[:, kps, PACK * CH * c : PACK * CH * (c + 1)]
+            nc.sync.dma_start(out=x_codes[c][:, kps, :].bitcast(I32), in_=src.bitcast(I32))
 
         def load_pool(g):
             by_slot = pool.rearrange("(g b t r) n -> g t b r n", g=2, t=PACK, r=8)
@@ -105,18 +105,20 @@ def tile_beam_power_log_bands_h2_kernel(
             out=cal_rows[0:PACK, :].rearrange("t (b r) -> t b r", r=8),
             in_=cal.rearrange("(b t r) -> t b r", t=PACK, r=8),
         )
-        load_w(RE0)
+        load_w(RE0, slice(0, 1))
         load_scales(ws_first, w_scales, 0, F)
         zero_plane(ws_rest)
         zero_plane(xs_rest)
-        load_x(0)
+        load_x(0, slice(0, 1))
         load_scales(xs_first, x_scales, 0, CH)
+        load_w(RE0, slice(1, 2))
+        load_x(0, slice(1, 2))
         load_w(RE1)
+        load_pool(0)
         load_scales(ws_rest, w_scales, F, D)
         load_w(IM0)
-        load_pool(0)
-        load_w(IM1)
         load_pool(1)
+        load_w(IM1)
         load_scales(xs_rest, x_scales, CH, M)
         load_x(1)
         nc.sync.dma_start(out=base_col[:], in_=base.rearrange("(p t) -> p t", t=PACK))
@@ -125,14 +127,20 @@ def tile_beam_power_log_bands_h2_kernel(
         load_x(2)
 
         def order_w(q):
+            order_w_planes(q)
+            order_w_codes(q)
+
+        def order_w_planes(q):
             raw_plane = (ws_first, ws_rest)[q // 2][:, :, CH * (q % 2) : CH * (q % 2 + 1)]
             nc.vector.tensor_copy(
                 out=w_planes[q][:].bitcast(I32).rearrange("p g (t b w) -> p g t b w", t=PACK, w=2),
                 in_=raw_plane.bitcast(I32).rearrange("p g (b t w) -> p g t b w", t=PACK, w=2),
             )
+
+        def order_w_codes(q, kps=slice(0, 2)):
             nc.vector.tensor_copy(
-                out=w_codes[q][:].bitcast(I32).rearrange("p g (t b w) -> p g t b w", t=PACK, w=4),
-                in_=w_raw[q][:].bitcast(I32).rearrange("p g (b t w) -> p g t b w", t=PACK, w=4),
+                out=w_codes[q][:, kps, :].bitcast(I32).rearrange("p g (t b w) -> p g t b w", t=PACK, w=4),
+                in_=w_raw[q][:, kps, :].bitcast(I32).rearrange("p g (b t w) -> p g t b w", t=PACK, w=4),
             )
 
         def x_plane(c, g):
@@ -140,15 +148,19 @@ def tile_beam_power_log_bands_h2_kernel(
 
         squares = {}
 
-        def beam(c, j, cuts=((0, CH),)):
+        beams = {}
+
+        def beam(c, j, cuts=((0, CH),), kps=(0, 1)):
             g, part, t = j // 8, (j // 4) % 2, j % 4
             q = 2 * part + g
-            if t == 0:
-                squares[(c, g, part)] = work.tile(
-                    [P, PACK, CH], F32, name="sq%d" % part, tag="sq%d" % part, bufs=3, align_bytes=64
-                )
-            z = psum_mm.tile([P, CH], F32, name="mm", tag="mm")
-            for kp in range(2):
+            if 0 in kps:
+                if t == 0:
+                    squares[(c, g, part)] = work.tile(
+                        [P, PACK, CH], F32, name="sq%d" % part, tag="sq%d" % part, bufs=3, align_bytes=64
+                    )
+                beams[(c, j)] = psum_mm.tile([P, CH], F32, name="mm", tag="mm")
+            z = beams[(c, j)]
+            for kp in kps:
                 nc.tensor.matmul_mx(
                     out=z[:],
                     lhsT=w_codes[q][:, kp, 2 * P * t : 2 * P * (t + 1)].bitcast(FP4X4),
@@ -159,7 +171,7 @@ def tile_beam_power_log_bands_h2_kernel(
                     stop=(kp == 1),
                 )
             col = PACK * g + t
-            for m0, m1 in cuts:
+            for m0, m1 in cuts if 1 in kps else ():
                 nc.scalar.activation(
                     out=squares[(c, g, part)][:, t, m0:m1],
                     in_=z[:, m0:m1],
@@ -189,10 +201,11 @@ def tile_beam_power_log_bands_h2_kernel(
                 in_=h_bf[(c, g)][:, PACK * m0 : PACK * m1],
             )
 
-        def group_pool(g):
+        def group_pool(g, half):
+            pairs = slice(32 * half, 32 * (half + 1))
             nc.vector.tensor_copy(
-                out=pool_grouped[g][:].rearrange("p (u m t) -> p m u t", u=PACK, t=PACK),
-                in_=pool_raw[g][:].rearrange("p t (m u) -> p m u t", u=PACK),
+                out=pool_grouped[g][:].rearrange("p (u c i t) -> p c t i u", u=PACK, i=2, t=PACK)[:, pairs],
+                in_=pool_raw[g][:].rearrange("p t (c i u) -> p c t i u", i=2, u=PACK)[:, pairs],
             )
 
         def sign_pool(g):
@@ -316,59 +329,72 @@ def tile_beam_power_log_bands_h2_kernel(
         nc.scalar.activation(out=cal_root[:], in_=cal_abs[:].rearrange("p g t -> p (g t)"), func=ACT.Sqrt)
         nc.scalar.activation(out=warm_ln[:], in_=one[:], func=ACT.Ln)
 
-        order_w(RE0)
+        order_w_codes(RE0, slice(0, 1))
+        order_w_planes(RE0)
         nc.vector.tensor_scalar(
             out=cal_step[:], in0=cal_t[:, :, 0:PACK], scalar1=0.0, scalar2=2.0, op0=ALU.is_ge, op1=ALU.mult
         )
-        for j in range(4):
+        order_w_codes(RE0, slice(1, 2))
+        for j in range(3):
+            beam(0, j, kps=(0,))
+        for j in range(3):
+            beam(0, j, kps=(1,))
+        for j in range(3, 4):
             beam(0, j)
         order_w(RE1)
         nc.vector.tensor_scalar(
             out=cal_sign[:], in0=cal_step[:], scalar1=1.0, scalar2=None, op0=ALU.subtract
         )
-        order_w(IM0)
-        for j in (8, 9, 10, 11, 4, 5, 6, 7):
+        for j in range(8, 12):
             beam(0, j)
         sign_pool(0)
+        group_pool(0, 0)
+        order_w(IM0)
+        for j in range(4, 8):
+            beam(0, j)
+        group_pool(0, 1)
+        sign_pool(1)
         order_w(IM1)
         for j in range(12, 16):
             beam(0, j)
-        group_pool(0)
-        sign_pool(1)
         quantize_pool(0)
-        group_pool(1)
+        group_pool(1, 0)
+        group_pool(1, 1)
         power(0, 0)
         quantize_pool(1)
         power(0, 1)
         quantize_h(0, 0)
         quantize_h(0, 1)
 
-        for j in range(10):
+        for j in range(12):
             beam(1, j)
         power(1, 0)
         for u in range(PACK):
             bands(0, u)
-            beam(1, 10 + u)
-        for j in range(10 + 4, 16):
+            if 12 + u < 16:
+                beam(1, 12 + u)
+        for j in range(12 + 4, 16):
             beam(1, j)
         affine(0, slots=(0, 1))
         quantize_h(1, 0)
         affine(0, slots=(2, 3))
-        turn(0, 0, 2 * P)
-        store_rows(0, 0, True)
-        group_y(0)
         power(1, 1)
+        group_y(0)
+        quantize_h(1, 1)
         quantize_y(0)
         store_codes(0)
-        quantize_h(1, 1)
-        store_rows(0, P, False)
 
-        for j in range(3):
+        for j in range(2):
+            beam(2, j)
+        turn(0, 0, 2 * P)
+        store_rows(0, 0, True)
+        store_rows(0, P, False)
+        for j in range(2, 6):
             beam(2, j)
         turn(0, 2 * P, CH)
-        store_rows(0, 2 * P, False)
+        store_rows(0, 2 * P, True)
         store_rows(0, 3 * P, False)
-        for j in range(3, 8):
+        for j in range(6, 8):
             beam(2, j)
         for u in range(PACK):
             bands(1, u)

@@ -18,8 +18,9 @@ ALU = mybir.AluOpType
 
 P = 128
 PACK = 4
-CH = 512
+BANK = 512
 RE0, RE1, IM0, IM1 = 0, 1, 2, 3
+CHUNKS = ((0, 512), (512, 512), (1024, 256), (1280, 256))
 
 
 def tile_beam_power_log_bands_h2_kernel(
@@ -29,183 +30,195 @@ def tile_beam_power_log_bands_h2_kernel(
     with ExitStack() as ctx:
         keep = ctx.enter_context(tc.tile_pool(name="keep", bufs=1))
         work = ctx.enter_context(tc.tile_pool(name="work", bufs=2))
-        psum_mm = ctx.enter_context(tc.psum_pool(name="psum_mm", bufs=4))
-        psum_tr = ctx.enter_context(tc.psum_pool(name="psum_tr", bufs=4))
+        psum = ctx.enter_context(tc.psum_pool(name="psum", bufs=8))
         ctx.enter_context(tc.manual_schedule())
 
         def kept(name, shape, dtype):
             return keep.tile(shape, dtype, name=name, align_bytes=64)
 
-        ws_first = kept("ws_first", [P, 2, F], U8)
-        ws_rest = kept("ws_rest", [P, 2, F], U8)
-        xs_first = kept("xs_first", [P, 2, CH], U8)
-        xs_rest = kept("xs_rest", [P, 2, 2 * CH], U8)
-        cal_rows = kept("cal_rows", [P, 2 * P], BF16)
-        one = kept("one", [P, 1], F32)
-        warm_sqrt = kept("warm_sqrt", [P, 1], F32)
+        def new_bank(shape):
+            return psum.tile(shape, F32, name="bank", tag="bank")
+
+        ws_re = kept("ws_re", [P, 2, F], U8)
+        ws_im = kept("ws_im", [P, 2, F], U8)
+        xs_first = kept("xs_first", [P, 2, BANK], U8)
+        xs_rest = kept("xs_rest", [P, 2, 2 * BANK], U8)
         warm_ln = kept("warm_ln", [P, 1], F32)
         warm_bf = kept("warm_bf", [P, PACK * P], BF16)
         warm_codes = kept("warm_codes", [P, P], U32)
         warm_plane = kept("warm_plane", [P, P], U8)
-        ident_bf = kept("ident_bf", [P, P], BF16)
-        ident_f32 = kept("ident_f32", [P, P], F32)
+        half = kept("half", [P, 2 * PACK], F32)
+        ident = kept("ident", [P, P], F32)
         base_col = kept("base_col", [P, PACK], BF16)
         gamma_col = kept("gamma_col", [P, PACK], BF16)
         beta_col = kept("beta_col", [P, PACK], BF16)
-        cal_abs = kept("cal_abs", [P, 2, PACK], F32)
+        cal_rows = kept("cal_rows", [P, 2 * P], BF16)
+        cal_dealt = kept("cal_dealt", [P, 2 * P], BF16)
+        cal_turned = kept("cal_turned", [P, 2 * PACK, 32], BF16)
+        cal_abs = kept("cal_abs", [P, 2 * PACK], F32)
         cal_root = kept("cal_root", [P, 2 * PACK], F32)
-        cal_step = kept("cal_step", [P, 2, PACK], F32)
-        cal_sign = kept("cal_sign", [P, 2, PACK], BF16)
-        w_raw = [kept("w_raw%d" % q, [P, 2, 2 * CH], U8) for q in range(4)]
-        w_codes = [kept("w_codes%d" % q, [P, 2, 2 * CH], U8) for q in range(4)]
-        w_planes = [kept("w_planes%d" % q, [P, 2, CH], U8) for q in range(4)]
-        x_codes = [kept("x_codes%d" % c, [P, 2, CH], U32) for c in range(3)]
+        cal_step = kept("cal_step", [P, 2 * PACK], F32)
+        cal_sign = kept("cal_sign", [P, 2 * PACK], F32)
+        w_raw = [kept("w_raw%d" % q, [P, 2, 2 * BANK], U8) for q in range(4)]
+        w_codes = [kept("w_codes%d" % q, [P, 2, 2 * BANK], U8) for q in range(4)]
+        w_planes = [kept("w_planes%d" % q, [P, 2, BANK], U8) for q in range(4)]
+        x_codes = [kept("x_codes%d" % i, [P, 2, BANK], U32) for i in range(3)]
         pool_raw = [kept("pool_raw%d" % g, [P, PACK, N], BF16) for g in range(2)]
         pool_grouped = [kept("pool_grouped%d" % g, [P, N * PACK], BF16) for g in range(2)]
         pool_codes = [kept("pool_codes%d" % g, [P, N], U32) for g in range(2)]
         pool_planes = [kept("pool_planes%d" % g, [P, N], U8) for g in range(2)]
-        y_codes = [kept("y_codes%d" % c, [P, CH], U32) for c in range(3)]
+        y_codes = [kept("y_codes%d" % c, [P, width], U32) for c, (first, width) in enumerate(CHUNKS)]
         y_plane = kept("y_plane", [P, M], U8)
 
         def zero_plane(plane):
             nc.vector.memset(plane[:].bitcast(I32), 0)
 
-        def load_scales(plane, scales, col0, col1, rows=range(4)):
+        def load_scales(plane, scales, col0, col1, rows=range(4), queue=nc.sync):
             by_row = scales.rearrange("g (q r) n -> r q g n", r=4)
             for r in rows:
-                nc.sync.dma_start(
+                queue.dma_start(
                     out=plane[r:P:32, :, :].bitcast(I32),
                     in_=by_row[r][:, :, col0:col1].bitcast(I32),
                 )
 
-        def load_w(q, kps=slice(0, 2)):
-            src = w_words.rearrange("g p b -> p g b")[:, kps, 2 * CH * q : 2 * CH * (q + 1)]
-            nc.sync.dma_start(out=w_raw[q][:, kps, :].bitcast(I32), in_=src.bitcast(I32))
+        def load_w(q, queue=nc.sync):
+            src = w_words.rearrange("g p b -> p g b")[:, :, 2 * BANK * q : 2 * BANK * (q + 1)]
+            queue.dma_start(out=w_raw[q][:].bitcast(I32), in_=src.bitcast(I32))
 
-        def load_x(c, kps=slice(0, 2)):
-            src = x_words.rearrange("g p m t -> p g (m t)")[:, kps, PACK * CH * c : PACK * CH * (c + 1)]
-            nc.sync.dma_start(out=x_codes[c][:, kps, :].bitcast(I32), in_=src.bitcast(I32))
+        def load_x(i, kps=slice(0, 2), queue=nc.sync):
+            src = x_words.rearrange("g p m t -> p g (m t)")[:, kps, PACK * BANK * i : PACK * BANK * (i + 1)]
+            queue.dma_start(out=x_codes[i][:, kps, :].bitcast(I32), in_=src.bitcast(I32))
 
         def load_pool(g):
             by_slot = pool.rearrange("(g b t r) n -> g t b r n", g=2, t=PACK, r=8)
             for t in range(PACK):
                 nc.sync.dma_start(out=pool_raw[g][:, t, :], in_=by_slot[g][t])
 
-        nc.gpsimd.memset(cal_rows[:].bitcast(I32), 0)
-        nc.gpsimd.memset(ws_first[:].bitcast(I32), 0)
-        nc.vector.memset(one[:], 1.0)
-        nc.vector.memset(warm_bf[:], 1.0)
-        zero_plane(xs_first)
-        nc.scalar.activation(out=warm_sqrt[:], in_=one[:], func=ACT.Sqrt)
-        make_identity(nc, ident_bf[:])
-        make_identity(nc, ident_f32[:])
-        nc.vector.quantize_mx(out=warm_codes[:].bitcast(FP8X4), scales=warm_plane[:], in_=warm_bf[:])
+        def load_cal():
+            nc.sync.dma_start(
+                out=cal_rows[0:P:32, :].rearrange("q (g c) -> q g c", g=2),
+                in_=cal.rearrange("(g q c) -> q g c", g=2, q=4),
+            )
 
-        nc.sync.dma_start(
-            out=cal_rows[0:PACK, :].rearrange("t (b r) -> t b r", r=8),
-            in_=cal.rearrange("(b t r) -> t b r", t=PACK, r=8),
-        )
-        load_w(RE0, slice(0, 1))
-        load_scales(ws_first, w_scales, 0, F)
-        zero_plane(ws_rest)
-        zero_plane(xs_rest)
-        load_x(0, slice(0, 1))
-        load_scales(xs_first, x_scales, 0, CH)
-        load_w(RE0, slice(1, 2))
-        load_x(0, slice(1, 2))
-        load_w(RE1)
-        load_pool(0)
-        load_scales(ws_rest, w_scales, F, D)
-        load_w(IM0)
-        load_pool(1)
-        load_w(IM1)
-        load_scales(xs_rest, x_scales, CH, M)
-        load_x(1)
-        nc.sync.dma_start(out=base_col[:], in_=base.rearrange("(p t) -> p t", t=PACK))
-        nc.sync.dma_start(out=gamma_col[:], in_=gamma.rearrange("(p t) -> p t", t=PACK))
-        nc.sync.dma_start(out=beta_col[:], in_=beta.rearrange("(p t) -> p t", t=PACK))
-        load_x(2)
+        def load_band_column(col, vec):
+            nc.sync.dma_start(out=col[:], in_=vec.rearrange("(p t) -> p t", t=PACK))
 
-        def order_w(q):
-            order_w_planes(q)
-            order_w_codes(q)
+        def deal_cal():
+            nc.vector.tensor_copy(
+                out=cal_dealt[:].rearrange("p (g t b r) -> p g t b r", g=2, t=PACK, r=8),
+                in_=cal_rows[:].rearrange("p (g b t r) -> p g t b r", g=2, t=PACK, r=8),
+            )
+
+        def turn_cal():
+            nc.vector.transpose(out=cal_turned[:].rearrange("p j c -> p (j c)"), in_=cal_dealt[:])
+
+        def root_of_cal():
+            values = cal_turned[:, :, 0]
+            nc.vector.scalar_tensor_tensor(
+                out=cal_abs[:], in0=values, scalar=-1.0, in1=values, op0=ALU.mult, op1=ALU.max
+            )
+            for cols in (slice(0, 1), slice(1, PACK), slice(PACK, 2 * PACK)):
+                nc.gpsimd.tensor_tensor(out=cal_root[:, cols], in0=cal_abs[:, cols], in1=half[:, cols], op=ALU.pow)
+
+        def step_of_cal():
+            nc.vector.tensor_scalar(
+                out=cal_step[:], in0=cal_turned[:, :, 0], scalar1=0.0, scalar2=2.0, op0=ALU.is_ge, op1=ALU.mult
+            )
+
+        def sign_of_cal():
+            nc.vector.tensor_scalar(out=cal_sign[:], in0=cal_step[:], scalar1=1.0, scalar2=None, op0=ALU.subtract)
 
         def order_w_planes(q):
-            raw_plane = (ws_first, ws_rest)[q // 2][:, :, CH * (q % 2) : CH * (q % 2 + 1)]
+            raw_plane = (ws_re, ws_im)[q // 2][:, :, BANK * (q % 2) : BANK * (q % 2 + 1)]
             nc.vector.tensor_copy(
                 out=w_planes[q][:].bitcast(I32).rearrange("p g (t b w) -> p g t b w", t=PACK, w=2),
                 in_=raw_plane.bitcast(I32).rearrange("p g (b t w) -> p g t b w", t=PACK, w=2),
             )
 
-        def order_w_codes(q, kps=slice(0, 2)):
+        def order_w_codes(q):
             nc.vector.tensor_copy(
-                out=w_codes[q][:, kps, :].bitcast(I32).rearrange("p g (t b w) -> p g t b w", t=PACK, w=4),
-                in_=w_raw[q][:, kps, :].bitcast(I32).rearrange("p g (b t w) -> p g t b w", t=PACK, w=4),
+                out=w_codes[q][:].bitcast(I32).rearrange("p g (t b w) -> p g t b w", t=PACK, w=4),
+                in_=w_raw[q][:].bitcast(I32).rearrange("p g (b t w) -> p g t b w", t=PACK, w=4),
             )
 
-        def x_plane(c, g):
-            return xs_first[:, g, :] if c == 0 else xs_rest[:, g, CH * (c - 1) : CH * c]
+        def order_w(q):
+            order_w_codes(q)
+            order_w_planes(q)
 
-        squares = {}
+        def x_operand(first, width, kp):
+            i, m0 = divmod(first, BANK)
+            plane = xs_first[:, kp, m0 : m0 + width] if i == 0 else xs_rest[:, kp, first - BANK : first - BANK + width]
+            return x_codes[i][:, kp, m0 : m0 + width].bitcast(FP8X4), plane
 
-        beams = {}
-
-        def beam(c, j, cuts=((0, CH),), kps=(0, 1)):
-            g, part, t = j // 8, (j // 4) % 2, j % 4
-            q = 2 * part + g
-            if 0 in kps:
-                if t == 0:
-                    squares[(c, g, part)] = work.tile(
-                        [P, PACK, CH], F32, name="sq%d" % part, tag="sq%d" % part, bufs=3, align_bytes=64
-                    )
-                beams[(c, j)] = psum_mm.tile([P, CH], F32, name="mm", tag="mm")
-            z = beams[(c, j)]
-            for kp in kps:
+        def beam_passes(out, first, width, q, t):
+            for kp in range(2):
+                codes, plane = x_operand(first, width, kp)
                 nc.tensor.matmul_mx(
-                    out=z[:],
+                    out=out,
                     lhsT=w_codes[q][:, kp, 2 * P * t : 2 * P * (t + 1)].bitcast(FP4X4),
                     lhsT_scale=w_planes[q][:, kp, P * t : P * (t + 1)],
-                    rhs=x_codes[c][:, kp, :].bitcast(FP8X4),
-                    rhs_scale=x_plane(c, kp),
+                    rhs=codes,
+                    rhs_scale=plane,
                     start=(kp == 0),
                     stop=(kp == 1),
                 )
-            col = PACK * g + t
-            for m0, m1 in cuts if 1 in kps else ():
-                nc.scalar.activation(
-                    out=squares[(c, g, part)][:, t, m0:m1],
-                    in_=z[:, m0:m1],
-                    func=ACT.Square,
-                    scale=cal_root[:, col : col + 1],
+
+        squares = {}
+
+        def squares_of(c, g):
+            if (c, g) not in squares:
+                squares[(c, g)] = work.tile(
+                    [P, 2, PACK, CHUNKS[c][1]], F32, name="squares", tag="squares", bufs=3, align_bytes=64
                 )
+            return squares[(c, g)]
+
+        def span(c, m0, m1):
+            return m0, (CHUNKS[c][1] if m1 is None else m1)
+
+        def beam(c, g, t, parts, m0, m1):
+            bank = new_bank([P, len(parts), m1 - m0])
+            for i, part in enumerate(parts):
+                beam_passes(bank[:, i, :], CHUNKS[c][0] + m0, m1 - m0, 2 * part + g, t)
+            nc.scalar.activation(
+                out=squares_of(c, g)[:, parts[0] : parts[-1] + 1, t, m0:m1],
+                in_=bank[:],
+                func=ACT.Square,
+                scale=cal_root[:, PACK * g + t : PACK * g + t + 1],
+            )
+
+        def beams(c, j0, j1):
+            for j in range(j0, j1):
+                beam(c, j // 8, j % 4, ((j // 4) % 2,), 0, BANK)
+
+        def narrow_beams(c, g, m0, m1, slots=range(PACK)):
+            for t in slots:
+                beam(c, g, t, (0, 1), m0, m1)
 
         h_bf, h_codes, h_planes = {}, {}, {}
 
-        def power(c, g, m0=0, m1=CH):
+        def power(c, g, m0=0, m1=None):
+            m0, m1 = span(c, m0, m1)
             if m0 == 0:
-                h_bf[(c, g)] = work.tile([P, CH * PACK], BF16, name="h_bf", tag="h_bf", bufs=2, align_bytes=64)
+                h_bf[(c, g)] = work.tile(
+                    [P, CHUNKS[c][1] * PACK], BF16, name="h_bf", tag="h_bf", bufs=2, align_bytes=64
+                )
             nc.vector.tensor_tensor(
                 out=h_bf[(c, g)][:, PACK * m0 : PACK * m1].rearrange("p (c i t) -> p c t i", i=4, t=PACK),
-                in0=squares[(c, g, 0)][:, :, m0:m1].rearrange("p t (c i) -> p c t i", i=4),
-                in1=squares[(c, g, 1)][:, :, m0:m1].rearrange("p t (c i) -> p c t i", i=4),
+                in0=squares[(c, g)][:, 0, :, m0:m1].rearrange("p t (c i) -> p c t i", i=4),
+                in1=squares[(c, g)][:, 1, :, m0:m1].rearrange("p t (c i) -> p c t i", i=4),
                 op=ALU.add,
             )
 
-        def quantize_h(c, g, m0=0, m1=CH):
+        def quantize_h(c, g, m0=0, m1=None):
+            m0, m1 = span(c, m0, m1)
             if m0 == 0:
-                h_codes[(c, g)] = work.tile([P, CH], U32, name="h_codes", tag="h_codes", bufs=4, align_bytes=64)
-                h_planes[(c, g)] = work.tile([P, CH], U8, name="h_plane", tag="h_plane", bufs=4, align_bytes=64)
+                width = CHUNKS[c][1]
+                h_codes[(c, g)] = work.tile([P, width], U32, name="h_codes", tag="h_codes", bufs=4, align_bytes=64)
+                h_planes[(c, g)] = work.tile([P, width], U8, name="h_plane", tag="h_plane", bufs=4, align_bytes=64)
             nc.vector.quantize_mx(
                 out=h_codes[(c, g)][:, m0:m1].bitcast(FP8X4),
                 scales=h_planes[(c, g)][:, m0:m1],
                 in_=h_bf[(c, g)][:, PACK * m0 : PACK * m1],
-            )
-
-        def group_pool(g, half):
-            pairs = slice(32 * half, 32 * (half + 1))
-            nc.vector.tensor_copy(
-                out=pool_grouped[g][:].rearrange("p (u c i t) -> p c t i u", u=PACK, i=2, t=PACK)[:, pairs],
-                in_=pool_raw[g][:].rearrange("p t (c i u) -> p c t i u", i=2, u=PACK)[:, pairs],
             )
 
         def sign_pool(g):
@@ -213,37 +226,65 @@ def tile_beam_power_log_bands_h2_kernel(
                 nc.vector.tensor_scalar(
                     out=pool_raw[g][:, t, :],
                     in0=pool_raw[g][:, t, :],
-                    scalar1=cal_sign[:, g, t : t + 1],
+                    scalar1=cal_sign[:, PACK * g + t : PACK * g + t + 1],
                     scalar2=None,
                     op0=ALU.mult,
                 )
+
+        def group_pool(g, part):
+            pairs = slice(32 * part, 32 * (part + 1))
+            nc.vector.tensor_copy(
+                out=pool_grouped[g][:].rearrange("p (u c i t) -> p c t i u", u=PACK, i=2, t=PACK)[:, pairs],
+                in_=pool_raw[g][:].rearrange("p t (c i u) -> p c t i u", i=2, u=PACK)[:, pairs],
+            )
 
         def quantize_pool(g):
             nc.vector.quantize_mx(
                 out=pool_codes[g][:].bitcast(FP8X4), scales=pool_planes[g][:], in_=pool_grouped[g][:]
             )
 
-        logs, ys, y_bf = {}, {}, {}
+        logs, ys, y_bf, energy = {}, {}, {}, {}
 
-        def bands(c, u, m0=0, m1=CH):
-            if u == 0 and m0 == 0:
-                logs[c] = work.tile([P, PACK, CH], F32, name="logs", tag="logs", bufs=2, align_bytes=64)
-            e = psum_mm.tile([P, m1 - m0], F32, name="mm", tag="mm")
-            for g in range(2):
-                nc.tensor.matmul_mx(
-                    out=e[:],
-                    lhsT=pool_codes[g][:, P * u : P * (u + 1)].bitcast(FP8X4),
-                    lhsT_scale=pool_planes[g][:, P * u : P * (u + 1)],
-                    rhs=h_codes[(c, g)][:, m0:m1].bitcast(FP8X4),
-                    rhs_scale=h_planes[(c, g)][:, m0:m1],
-                    start=(g == 0),
-                    stop=(g == 1),
-                )
-            nc.scalar.activation(out=logs[c][:, u, m0:m1], in_=e[:], func=ACT.Ln, bias=base_col[:, u : u + 1])
+        def band_pass(out, c, g, u, m0, m1, start, stop):
+            nc.tensor.matmul_mx(
+                out=out,
+                lhsT=pool_codes[g][:, P * u : P * (u + 1)].bitcast(FP8X4),
+                lhsT_scale=pool_planes[g][:, P * u : P * (u + 1)],
+                rhs=h_codes[(c, g)][:, m0:m1].bitcast(FP8X4),
+                rhs_scale=h_planes[(c, g)][:, m0:m1],
+                start=start,
+                stop=stop,
+            )
 
-        def affine(c, m0=0, m1=CH, slots=range(PACK)):
-            if m0 == 0 and 0 in slots:
-                ys[c] = work.tile([P, PACK, CH], F32, name="ys", tag="ys", bufs=2, align_bytes=64)
+        def take_log(c, u, m0, m1, src):
+            if c not in logs:
+                logs[c] = work.tile([P, PACK, CHUNKS[c][1]], F32, name="logs", tag="logs", bufs=2, align_bytes=64)
+            nc.scalar.activation(out=logs[c][:, u, m0:m1], in_=src, func=ACT.Ln, bias=base_col[:, u : u + 1])
+
+        def bands(c, slots, m0=0, m1=None):
+            m0, m1 = span(c, m0, m1)
+            bank = new_bank([P, len(slots), m1 - m0])
+            for i, u in enumerate(slots):
+                for g in range(2):
+                    band_pass(bank[:, i, :], c, g, u, m0, m1, g == 0, g == 1)
+            for i, u in enumerate(slots):
+                take_log(c, u, m0, m1, bank[:, i, :])
+
+        def bands_open(c, slots, m0, m1):
+            energy[(c, slots, m0)] = new_bank([P, len(slots), m1 - m0])
+            for i, u in enumerate(slots):
+                band_pass(energy[(c, slots, m0)][:, i, :], c, 0, u, m0, m1, i == 0, False)
+
+        def bands_close(c, slots, m0, m1):
+            for i, u in enumerate(slots):
+                band_pass(energy[(c, slots, m0)][:, i, :], c, 1, u, m0, m1, False, i == len(slots) - 1)
+            for i, u in enumerate(slots):
+                take_log(c, u, m0, m1, energy[(c, slots, m0)][:, i, :])
+
+        def affine(c, slots=range(PACK), m0=0, m1=None):
+            m0, m1 = span(c, m0, m1)
+            if c not in ys:
+                ys[c] = work.tile([P, PACK, CHUNKS[c][1]], F32, name="ys", tag="ys", bufs=2, align_bytes=64)
             for u in slots:
                 nc.vector.tensor_scalar(
                     out=ys[c][:, u, m0:m1],
@@ -254,61 +295,55 @@ def tile_beam_power_log_bands_h2_kernel(
                     op1=ALU.add,
                 )
 
-        def group_y(c, m0=0, m1=CH):
+        def group_y(c, m0=0, m1=None):
+            m0, m1 = span(c, m0, m1)
             if m0 == 0:
-                y_bf[c] = work.tile([P, CH * PACK], BF16, name="y_bf", tag="y_bf", bufs=2, align_bytes=64)
+                y_bf[c] = work.tile([P, CHUNKS[c][1] * PACK], BF16, name="y_bf", tag="y_bf", bufs=2, align_bytes=64)
             nc.vector.tensor_copy(
                 out=y_bf[c][:, PACK * m0 : PACK * m1].rearrange("p (c i u) -> p c u i", i=4, u=PACK),
                 in_=ys[c][:, :, m0:m1].rearrange("p u (c i) -> p c u i", i=4),
             )
 
-        def quantize_y(c, m0=0, m1=CH):
+        def quantize_y(c, m0=0, m1=None):
+            m0, m1 = span(c, m0, m1)
+            first = CHUNKS[c][0]
             nc.vector.quantize_mx(
                 out=y_codes[c][:, m0:m1].bitcast(FP8X4),
-                scales=y_plane[:, CH * c + m0 : CH * c + m1],
+                scales=y_plane[:, first + m0 : first + m1],
                 in_=y_bf[c][:, PACK * m0 : PACK * m1],
             )
-
-        def store_codes(c, m0=0, m1=CH):
-            dst = out_1[0].rearrange("p m t -> p (m t)")[:, PACK * (CH * c + m0) : PACK * (CH * c + m1)]
+            dst = out_1[0].rearrange("p m t -> p (m t)")[:, PACK * (first + m0) : PACK * (first + m1)]
             nc.sync.dma_start(out=dst.bitcast(I32), in_=y_codes[c][:, m0:m1].bitcast(I32))
+
+        def store_scales(col0, col1, queues=(nc.sync,) * 4):
+            for quad in range(4):
+                queues[quad].dma_start(
+                    out=out_2[0][4 * quad : 4 * quad + 4, col0:col1].bitcast(I32),
+                    in_=y_plane[32 * quad : 32 * quad + 4, col0:col1].bitcast(I32),
+                )
 
         turned = {}
 
-        def turn(c, m0=0, m1=CH):
+        def turn(c, m0=0, m1=None):
+            m0, m1 = span(c, m0, m1)
             for row0 in range(m0, m1, P):
-                bank = psum_tr.tile([P, PACK, P], F32, name="tr", tag="tr")
-                turned[(c, row0)] = bank
+                turned[(c, row0)] = new_bank([P, PACK, P])
                 for u in range(PACK):
-                    nc.tensor.transpose(bank[:, u, :], ys[c][:, u, row0 : row0 + P], ident_f32[:])
+                    nc.tensor.transpose(turned[(c, row0)][:, u, :], ys[c][:, u, row0 : row0 + P], ident[:])
 
-        def store_rows(c, row0, on_scalar, queue=nc.sync, tiles=1):
-            rows = work.tile([P, tiles, N], F32, name="rows", tag="rows", bufs=6, align_bytes=64)
-            for i in range(tiles):
-                dst = rows[:, i, :].rearrange("m (p u) -> m p u", u=PACK)
-                src = turned[(c, row0 + P * i)][:].rearrange("m u p -> m p u")
-                if on_scalar:
-                    nc.scalar.copy(out=dst, in_=src)
-                else:
-                    nc.vector.tensor_copy(out=dst, in_=src)
-            first = CH * c + row0
-            queue.dma_start(out=out_0[first : first + P * tiles, :].rearrange("(i m) n -> m i n", m=P), in_=rows[:])
-
-        def keep_warm(passes):
-            idle = psum_mm.tile([P, CH], F32, name="mm", tag="mm")
-            for i in range(passes):
-                nc.tensor.matmul_mx(
-                    out=idle[:],
-                    lhsT=warm_codes[:].bitcast(FP8X4),
-                    lhsT_scale=warm_plane[:],
-                    rhs=x_codes[0][:, 0, :].bitcast(FP8X4),
-                    rhs_scale=x_plane(0, 0),
-                    start=True,
-                    stop=True,
-                )
+        def store_rows(c, row0, on_scalar, queue=nc.sync):
+            rows = work.tile([P, N], F32, name="rows", tag="rows", bufs=6, align_bytes=64)
+            dst = rows[:].rearrange("m (p u) -> m p u", u=PACK)
+            src = turned[(c, row0)][:].rearrange("m u p -> m p u")
+            if on_scalar:
+                nc.scalar.copy(out=dst, in_=src)
+            else:
+                nc.vector.tensor_copy(out=dst, in_=src)
+            first = CHUNKS[c][0] + row0
+            queue.dma_start(out=out_0[first : first + P, :], in_=rows[:])
 
         def warm_tensor(passes):
-            idle = psum_mm.tile([P, P], F32, name="mm", tag="mm")
+            idle = new_bank([P, P])
             for i in range(passes):
                 nc.tensor.matmul_mx(
                     out=idle[:],
@@ -320,43 +355,54 @@ def tile_beam_power_log_bands_h2_kernel(
                     stop=True,
                 )
 
-        warm_tensor(8)
-        cal_t = psum_tr.tile([P, 2, P], BF16, name="tr", tag="tr")
-        for g in range(2):
-            nc.tensor.transpose(cal_t[:, g, :], cal_rows[:, P * g : P * (g + 1)], ident_bf[:])
-        warm_tensor(8)
-        nc.scalar.activation(out=cal_abs[:], in_=cal_t[:, :, 0:PACK], func=ACT.Abs)
-        nc.scalar.activation(out=cal_root[:], in_=cal_abs[:].rearrange("p g t -> p (g t)"), func=ACT.Sqrt)
-        nc.scalar.activation(out=warm_ln[:], in_=one[:], func=ACT.Ln)
-
-        order_w_codes(RE0, slice(0, 1))
+        load_w(RE0, nc.scalar)
+        zero_plane(cal_rows)
+        zero_plane(ws_re)
+        zero_plane(xs_first)
+        nc.vector.memset(warm_bf[:].bitcast(F32), 1.0)
+        zero_plane(ws_im)
+        nc.vector.quantize_mx(out=warm_codes[:].bitcast(FP8X4), scales=warm_plane[:], in_=warm_bf[:])
+        zero_plane(xs_rest)
+        nc.vector.memset(ident[:], 0.0)
+        nc.gpsimd.memset(half[:], 0.5)
+        make_identity(nc, ident[:], nomemset=True)
+        load_cal()
+        load_scales(ws_re, w_scales, 0, F)
+        load_x(0)
+        nc.scalar.activation(out=warm_ln[:], in_=half[:, 0:1], func=ACT.Ln)
+        load_scales(xs_first, x_scales, 0, BANK)
+        load_w(RE1)
+        load_pool(0)
+        load_scales(ws_im, w_scales, F, D)
+        load_w(IM0)
+        load_pool(1)
+        load_w(IM1)
+        load_scales(xs_rest, x_scales, BANK, M)
+        load_x(1)
+        load_band_column(base_col, base)
+        load_band_column(gamma_col, gamma)
+        load_band_column(beta_col, beta)
+        load_x(2)
+        warm_tensor(16)
+        deal_cal()
+        order_w_codes(RE0)
+        turn_cal()
+        root_of_cal()
         order_w_planes(RE0)
-        nc.vector.tensor_scalar(
-            out=cal_step[:], in0=cal_t[:, :, 0:PACK], scalar1=0.0, scalar2=2.0, op0=ALU.is_ge, op1=ALU.mult
-        )
-        order_w_codes(RE0, slice(1, 2))
-        for j in range(3):
-            beam(0, j, kps=(0,))
-        for j in range(3):
-            beam(0, j, kps=(1,))
-        for j in range(3, 4):
-            beam(0, j)
+        step_of_cal()
+        sign_of_cal()
+
+        beams(0, 0, 4)
         order_w(RE1)
-        nc.vector.tensor_scalar(
-            out=cal_sign[:], in0=cal_step[:], scalar1=1.0, scalar2=None, op0=ALU.subtract
-        )
-        for j in range(8, 12):
-            beam(0, j)
+        beams(0, 8, 12)
         sign_pool(0)
         group_pool(0, 0)
         order_w(IM0)
-        for j in range(4, 8):
-            beam(0, j)
+        beams(0, 4, 8)
         group_pool(0, 1)
-        sign_pool(1)
         order_w(IM1)
-        for j in range(12, 16):
-            beam(0, j)
+        sign_pool(1)
+        beams(0, 12, 16)
         quantize_pool(0)
         group_pool(1, 0)
         group_pool(1, 1)
@@ -366,106 +412,85 @@ def tile_beam_power_log_bands_h2_kernel(
         quantize_h(0, 0)
         quantize_h(0, 1)
 
-        for j in range(12):
-            beam(1, j)
+        HALF = 2 * P
+        ALL = tuple(range(PACK))
+        beams(1, 0, 8)
         power(1, 0)
+        narrow_beams(1, 1, 0, HALF, (0,))
         for u in range(PACK):
-            bands(0, u)
-            if 12 + u < 16:
-                beam(1, 12 + u)
-        for j in range(12 + 4, 16):
-            beam(1, j)
-        affine(0, slots=(0, 1))
+            bands(0, (u,))
+        affine(0)
         quantize_h(1, 0)
-        affine(0, slots=(2, 3))
-        power(1, 1)
-        group_y(0)
-        quantize_h(1, 1)
-        quantize_y(0)
-        store_codes(0)
-
-        for j in range(2):
-            beam(2, j)
-        turn(0, 0, 2 * P)
+        narrow_beams(1, 1, 0, HALF, (1, 2, 3))
+        turn(0, 0, HALF)
         store_rows(0, 0, True)
+        group_y(0)
         store_rows(0, P, False)
-        for j in range(2, 6):
-            beam(2, j)
-        turn(0, 2 * P, CH)
+        power(1, 1, 0, HALF)
+        narrow_beams(1, 1, HALF, BANK, (0, 1))
+        turn(0, HALF, BANK)
         store_rows(0, 2 * P, True)
+        quantize_y(0)
+        quantize_h(1, 1, 0, HALF)
         store_rows(0, 3 * P, False)
-        for j in range(6, 8):
-            beam(2, j)
-        for u in range(PACK):
-            bands(1, u)
-            beam(2, 8 + u)
+        narrow_beams(1, 1, HALF, BANK, (2, 3))
+
+        narrow_beams(2, 0, 0, HALF, (0,))
+        bands(1, (0, 1), 0, HALF)
+        bands(1, (2, 3), 0, HALF)
+        power(1, 1, HALF, BANK)
+        affine(1, ALL, 0, HALF)
+        quantize_h(1, 1, HALF, BANK)
+        narrow_beams(2, 0, 0, HALF, (1, 2, 3))
+        bands(1, (0, 1), HALF, BANK)
+        bands(1, (2, 3), HALF, BANK)
+        group_y(1, 0, HALF)
         power(2, 0)
-        for j in range(8 + 4, 14):
-            beam(2, j)
-        affine(1, slots=(0, 1))
-        quantize_h(2, 0)
-        affine(1, slots=(2, 3))
-        turn(1, 0, 2 * P)
+        narrow_beams(2, 1, 0, HALF, (0, 1))
+        turn(1, 0, HALF)
         store_rows(1, 0, True)
-        beam(2, 14)
-        beam(2, 15, ((0, P), (P, CH)))
-        group_y(1)
-        turn(1, 2 * P, CH)
-        keep_warm(2)
+        affine(1, ALL, HALF, BANK)
+        quantize_h(2, 0)
+        store_rows(1, P, False)
+        narrow_beams(2, 1, 0, HALF, (2, 3))
+        group_y(1, HALF, BANK)
         quantize_y(1)
-        store_codes(1)
-        for quad in range(4):
-            nc.sync.dma_start(
-                out=out_2[0][4 * quad : 4 * quad + 4, 0:1024].bitcast(I32),
-                in_=y_plane[32 * quad : 32 * quad + 4, 0:1024].bitcast(I32),
-            )
-        store_rows(1, 128, True)
-        store_rows(1, 256, True)
-        store_rows(1, 384, True)
-        power(2, 1, 0, 128)
-        power(2, 1, 128, 256)
-        quantize_h(2, 1, 0, 128)
-        power(2, 1, 256, 384)
-        quantize_h(2, 1, 128, 256)
-        power(2, 1, 384, 512)
-        quantize_h(2, 1, 256, 384)
-        bands(2, 0, 0, 128)
-        bands(2, 1, 0, 128)
-        bands(2, 2, 0, 128)
-        bands(2, 3, 0, 128)
-        bands(2, 0, 128, 256)
-        bands(2, 1, 128, 256)
-        bands(2, 2, 128, 256)
-        bands(2, 3, 128, 256)
-        affine(2, 0, 128)
-        quantize_h(2, 1, 384, 512)
-        bands(2, 0, 256, 384)
-        bands(2, 1, 256, 384)
-        bands(2, 2, 256, 384)
-        bands(2, 3, 256, 384)
-        bands(2, 0, 384, 512)
-        bands(2, 1, 384, 512)
-        bands(2, 2, 384, 512)
-        bands(2, 3, 384, 512)
-        turn(2, 0, 128)
-        affine(2, 128, 256)
-        turn(2, 128, 256)
-        group_y(2, 0, 256)
-        affine(2, 256, 384)
-        turn(2, 256, 384)
-        quantize_y(2, 0, 256)
-        store_codes(2, 0, 256)
-        affine(2, 384, 512)
-        turn(2, 384, 512)
+        power(2, 1)
+        quantize_h(2, 1)
+
+        narrow_beams(3, 0, 0, HALF)
+        narrow_beams(3, 1, 0, P, (0, 1))
+        bands(2, (0, 1))
+        bands(2, (2, 3))
+        power(3, 0)
+        affine(2)
+        quantize_h(3, 0)
+        narrow_beams(3, 1, 0, P, (2, 3))
+        group_y(2)
+        narrow_beams(3, 1, P, HALF)
+        power(3, 1, 0, P)
+        quantize_y(2)
+        store_scales(0, CHUNKS[3][0])
+        quantize_h(3, 1, 0, P)
+        turn(1, HALF, BANK)
+        turn(2)
+        store_rows(1, 2 * P, True)
+        store_rows(1, 3 * P, True)
         store_rows(2, 0, True)
-        store_rows(2, 128, True)
-        group_y(2, 256, 512)
-        store_rows(2, 256, True)
-        store_rows(2, 384, True, nc.scalar)
-        quantize_y(2, 256, 512)
-        store_codes(2, 256, 512)
-        for quad in range(4):
-            nc.sync.dma_start(
-                out=out_2[0][4 * quad : 4 * quad + 4, 1024:1536].bitcast(I32),
-                in_=y_plane[32 * quad : 32 * quad + 4, 1024:1536].bitcast(I32),
-            )
+        bands_open(3, ALL, 0, P)
+        bands_close(3, ALL, 0, P)
+        bands_open(3, ALL, P, HALF)
+        power(3, 1, P, HALF)
+        quantize_h(3, 1, P, HALF)
+        bands_close(3, ALL, P, HALF)
+        store_rows(2, P, False)
+        affine(3, ALL, 0, P)
+        turn(3, 0, P)
+        affine(3, ALL, P, HALF)
+        turn(3, P, HALF)
+        store_rows(3, 0, True)
+        group_y(3, 0, P)
+        group_y(3, P, HALF)
+        store_rows(3, P, True, nc.scalar)
+        quantize_y(3)
+        store_scales(CHUNKS[3][0], M)

@@ -284,7 +284,7 @@ def tile_beam_power_log_bands_h2_kernel(
         def affine(c, slots=range(PACK), m0=0, m1=None):
             m0, m1 = span(c, m0, m1)
             if c not in ys:
-                ys[c] = work.tile([P, PACK, CHUNKS[c][1]], F32, name="ys", tag="ys", bufs=2, align_bytes=64)
+                ys[c] = work.tile([P, PACK, CHUNKS[c][1]], F32, name="ys", tag="ys", bufs=3, align_bytes=64)
             for u in slots:
                 nc.vector.tensor_scalar(
                     out=ys[c][:, u, m0:m1],
@@ -341,6 +341,26 @@ def tile_beam_power_log_bands_h2_kernel(
                 nc.vector.tensor_copy(out=dst, in_=src)
             first = CHUNKS[c][0] + row0
             queue.dma_start(out=out_0[first : first + P, :], in_=rows[:])
+
+        y_blocks = kept("y_blocks", [P, PACK, BANK], F32)
+        y_rows = kept("y_rows", [P, BANK * PACK], F32)
+
+        def turn_blocks(c, u):
+            nc.vector.transpose(out=y_blocks[:, u, :], in_=ys[c][:, u, :])
+
+        def join_blocks(m0, m1):
+            nc.vector.tensor_copy(
+                out=y_rows[:, PACK * m0 : PACK * m1].rearrange("p (c i u) -> p c u i", i=2, u=PACK),
+                in_=y_blocks[:, :, m0:m1].rearrange("p u (c i) -> p c u i", i=2),
+            )
+
+        def store_blocks(c):
+            first = CHUNKS[c][0]
+            for quad in range(4):
+                nc.sync.dma_start(
+                    out=out_0[first : first + BANK, P * quad : P * (quad + 1)].rearrange("(j i) n -> i j n", i=32),
+                    in_=y_rows[32 * quad : 32 * (quad + 1), :].rearrange("i (j n) -> i j n", n=P),
+                )
 
         def warm_tensor(passes):
             idle = new_bank([P, P])
@@ -422,56 +442,58 @@ def tile_beam_power_log_bands_h2_kernel(
         affine(0)
         quantize_h(1, 0)
         narrow_beams(1, 1, 0, HALF, (1, 2, 3))
-        turn(0, 0, HALF)
-        store_rows(0, 0, True)
-        group_y(0)
-        store_rows(0, P, False)
+        turn_blocks(0, 0)
         power(1, 1, 0, HALF)
-        narrow_beams(1, 1, HALF, BANK, (0, 1))
-        turn(0, HALF, BANK)
-        store_rows(0, 2 * P, True)
-        quantize_y(0)
+        turn_blocks(0, 1)
         quantize_h(1, 1, 0, HALF)
-        store_rows(0, 3 * P, False)
-        narrow_beams(1, 1, HALF, BANK, (2, 3))
+        narrow_beams(1, 1, HALF, BANK)
+        turn_blocks(0, 2)
+        power(1, 1, HALF, BANK)
+        turn_blocks(0, 3)
+        quantize_h(1, 1, HALF, BANK)
 
         narrow_beams(2, 0, 0, HALF, (0,))
         bands(1, (0, 1), 0, HALF)
         bands(1, (2, 3), 0, HALF)
-        power(1, 1, HALF, BANK)
         affine(1, ALL, 0, HALF)
-        quantize_h(1, 1, HALF, BANK)
+        join_blocks(0, BANK)
+        store_blocks(0)
         narrow_beams(2, 0, 0, HALF, (1, 2, 3))
         bands(1, (0, 1), HALF, BANK)
         bands(1, (2, 3), HALF, BANK)
-        group_y(1, 0, HALF)
         power(2, 0)
+        group_y(0, 0, HALF)
         narrow_beams(2, 1, 0, HALF, (0, 1))
         turn(1, 0, HALF)
         store_rows(1, 0, True)
+        store_rows(1, P, True)
         affine(1, ALL, HALF, BANK)
         quantize_h(2, 0)
-        store_rows(1, P, False)
         narrow_beams(2, 1, 0, HALF, (2, 3))
-        group_y(1, HALF, BANK)
-        quantize_y(1)
+        group_y(0, HALF, BANK)
+        quantize_y(0)
         power(2, 1)
+        group_y(1, 0, HALF)
         quantize_h(2, 1)
+        group_y(1, HALF, BANK)
 
         narrow_beams(3, 0, 0, HALF)
-        narrow_beams(3, 1, 0, P, (0, 1))
+        narrow_beams(3, 1, 0, P, (0, 1, 2))
         bands(2, (0, 1))
         bands(2, (2, 3))
         power(3, 0)
-        affine(2)
+        quantize_y(1)
+        store_scales(0, CHUNKS[2][0])
         quantize_h(3, 0)
-        narrow_beams(3, 1, 0, P, (2, 3))
-        group_y(2)
+        affine(2)
+        narrow_beams(3, 1, 0, P, (3,))
         narrow_beams(3, 1, P, HALF)
         power(3, 1, 0, P)
-        quantize_y(2)
-        store_scales(0, CHUNKS[3][0])
+        group_y(2, 0, P)
         quantize_h(3, 1, 0, P)
+        power(3, 1, P, HALF)
+        group_y(2, P, HALF)
+        quantize_h(3, 1, P, HALF)
         turn(1, HALF, BANK)
         turn(2)
         store_rows(1, 2 * P, True)
@@ -480,10 +502,9 @@ def tile_beam_power_log_bands_h2_kernel(
         bands_open(3, ALL, 0, P)
         bands_close(3, ALL, 0, P)
         bands_open(3, ALL, P, HALF)
-        power(3, 1, P, HALF)
-        quantize_h(3, 1, P, HALF)
         bands_close(3, ALL, P, HALF)
         store_rows(2, P, False)
+        quantize_y(2)
         affine(3, ALL, 0, P)
         turn(3, 0, P)
         affine(3, ALL, P, HALF)
@@ -493,4 +514,4 @@ def tile_beam_power_log_bands_h2_kernel(
         group_y(3, P, HALF)
         store_rows(3, P, True, nc.scalar)
         quantize_y(3)
-        store_scales(CHUNKS[3][0], M)
+        store_scales(CHUNKS[2][0], M)

@@ -354,10 +354,10 @@ def tile_beam_power_log_bands_h2_kernel(
                 in_=y_blocks[:, :, m0:m1].rearrange("p u (c i) -> p c u i", i=2),
             )
 
-        def store_blocks(c):
+        def store_blocks(c, quads, queue):
             first = CHUNKS[c][0]
-            for quad in range(4):
-                nc.sync.dma_start(
+            for quad in quads:
+                queue.dma_start(
                     out=out_0[first : first + BANK, P * quad : P * (quad + 1)].rearrange("(j i) n -> i j n", i=32),
                     in_=y_rows[32 * quad : 32 * (quad + 1), :].rearrange("i (j n) -> i j n", n=P),
                 )
@@ -457,10 +457,11 @@ def tile_beam_power_log_bands_h2_kernel(
         bands(1, (2, 3), 0, HALF)
         affine(1, ALL, 0, HALF)
         join_blocks(0, BANK)
-        store_blocks(0)
+        store_blocks(0, (0, 1), nc.sync)
         narrow_beams(2, 0, 0, HALF, (1, 2, 3))
         bands(1, (0, 1), HALF, BANK)
         bands(1, (2, 3), HALF, BANK)
+        store_blocks(0, (2, 3), nc.scalar)
         power(2, 0)
         group_y(0, 0, HALF)
         narrow_beams(2, 1, 0, HALF, (0, 1))

@@ -94,8 +94,8 @@ def tile_beam_power_log_bands_h2_kernel(
             for t in range(PACK):
                 nc.sync.dma_start(out=pool_raw[g][:, t, :], in_=by_slot[g][t])
 
-        def load_cal():
-            nc.sync.dma_start(
+        def load_cal(queue):
+            queue.dma_start(
                 out=cal_rows[0:P:32, :].rearrange("q (g c) -> q g c", g=2),
                 in_=cal.rearrange("(g q c) -> q g c", g=2, q=4),
             )
@@ -312,8 +312,9 @@ def tile_beam_power_log_bands_h2_kernel(
                 scales=y_plane[:, first + m0 : first + m1],
                 in_=y_bf[c][:, PACK * m0 : PACK * m1],
             )
-            dst = out_1[0].rearrange("p m t -> p (m t)")[:, PACK * (first + m0) : PACK * (first + m1)]
-            nc.sync.dma_start(out=dst.bitcast(I32), in_=y_codes[c][:, m0:m1].bitcast(I32))
+            if m1 == CHUNKS[c][1]:
+                dst = out_1[0].rearrange("p m t -> p (m t)")[:, PACK * first : PACK * (first + m1)]
+                nc.sync.dma_start(out=dst.bitcast(I32), in_=y_codes[c][:].bitcast(I32))
 
         def store_scales(col0, col1, queues=(nc.sync,) * 4):
             for quad in range(4):
@@ -331,16 +332,19 @@ def tile_beam_power_log_bands_h2_kernel(
                 for u in range(PACK):
                     nc.tensor.transpose(turned[(c, row0)][:, u, :], ys[c][:, u, row0 : row0 + P], ident[:])
 
-        def store_rows(c, row0, on_scalar, queue=nc.sync):
+        def store_rows(c, row0, on_scalar, queues=(nc.sync,)):
             rows = work.tile([P, N], F32, name="rows", tag="rows", bufs=6, align_bytes=64)
-            dst = rows[:].rearrange("m (p u) -> m p u", u=PACK)
-            src = turned[(c, row0)][:].rearrange("m u p -> m p u")
-            if on_scalar:
-                nc.scalar.copy(out=dst, in_=src)
-            else:
-                nc.vector.tensor_copy(out=dst, in_=src)
             first = CHUNKS[c][0] + row0
-            queue.dma_start(out=out_0[first : first + P, :], in_=rows[:])
+            share = P // len(queues)
+            for i, queue in enumerate(queues):
+                cols = slice(PACK * share * i, PACK * share * (i + 1))
+                dst = rows[:, cols].rearrange("m (p u) -> m p u", u=PACK)
+                src = turned[(c, row0)][:, :, share * i : share * (i + 1)].rearrange("m u p -> m p u")
+                if on_scalar:
+                    nc.scalar.copy(out=dst, in_=src)
+                else:
+                    nc.vector.tensor_copy(out=dst, in_=src)
+                queue.dma_start(out=out_0[first : first + P, cols], in_=rows[:, cols])
 
         y_blocks = kept("y_blocks", [P, PACK, BANK], F32)
         y_rows = kept("y_rows", [P, BANK * PACK], F32)
@@ -362,22 +366,22 @@ def tile_beam_power_log_bands_h2_kernel(
                     in_=y_rows[32 * quad : 32 * (quad + 1), :].rearrange("i (j n) -> i j n", n=P),
                 )
 
-        def warm_tensor(passes):
+        def warm_tensor(passes, moving):
             idle = new_bank([P, P])
             for i in range(passes):
                 nc.tensor.matmul_mx(
                     out=idle[:],
                     lhsT=warm_codes[:].bitcast(FP8X4),
                     lhsT_scale=warm_plane[:],
-                    rhs=warm_codes[:].bitcast(FP8X4),
+                    rhs=moving.bitcast(FP8X4),
                     rhs_scale=warm_plane[:],
                     start=True,
                     stop=True,
                 )
 
         load_w(RE0, nc.scalar)
-        zero_plane(cal_rows)
-        zero_plane(ws_re)
+        nc.gpsimd.memset(ws_re[:].bitcast(I32), 0)
+        nc.gpsimd.memset(cal_rows[:].bitcast(I32), 0)
         zero_plane(xs_first)
         nc.vector.memset(warm_bf[:].bitcast(F32), 1.0)
         zero_plane(ws_im)
@@ -386,8 +390,9 @@ def tile_beam_power_log_bands_h2_kernel(
         nc.vector.memset(ident[:], 0.0)
         nc.gpsimd.memset(half[:], 0.5)
         make_identity(nc, ident[:], nomemset=True)
-        load_cal()
-        load_scales(ws_re, w_scales, 0, F)
+        load_scales(ws_re, w_scales, 0, F, rows=(0, 1))
+        load_cal(nc.sync)
+        load_scales(ws_re, w_scales, 0, F, rows=(2, 3))
         load_x(0)
         nc.scalar.activation(out=warm_ln[:], in_=half[:, 0:1], func=ACT.Ln)
         load_scales(xs_first, x_scales, 0, BANK)
@@ -403,7 +408,8 @@ def tile_beam_power_log_bands_h2_kernel(
         load_band_column(gamma_col, gamma)
         load_band_column(beta_col, beta)
         load_x(2)
-        warm_tensor(16)
+        warm_tensor(14, warm_codes[:])
+        warm_tensor(6, x_codes[0][:, 0, 0:P])
         deal_cal()
         order_w_codes(RE0)
         turn_cal()
@@ -452,13 +458,13 @@ def tile_beam_power_log_bands_h2_kernel(
         turn_blocks(0, 3)
         quantize_h(1, 1, HALF, BANK)
 
-        narrow_beams(2, 0, 0, HALF, (0,))
+        narrow_beams(2, 0, 0, HALF, (0, 1))
         bands(1, (0, 1), 0, HALF)
         bands(1, (2, 3), 0, HALF)
         affine(1, ALL, 0, HALF)
         join_blocks(0, BANK)
         store_blocks(0, (0, 1), nc.sync)
-        narrow_beams(2, 0, 0, HALF, (1, 2, 3))
+        narrow_beams(2, 0, 0, HALF, (2, 3))
         bands(1, (0, 1), HALF, BANK)
         bands(1, (2, 3), HALF, BANK)
         store_blocks(0, (2, 3), nc.scalar)
@@ -467,34 +473,35 @@ def tile_beam_power_log_bands_h2_kernel(
         narrow_beams(2, 1, 0, HALF, (0, 1))
         turn(1, 0, HALF)
         store_rows(1, 0, True)
-        store_rows(1, P, True)
         affine(1, ALL, HALF, BANK)
         quantize_h(2, 0)
         narrow_beams(2, 1, 0, HALF, (2, 3))
         group_y(0, HALF, BANK)
+        store_rows(1, P, False)
         quantize_y(0)
         power(2, 1)
-        group_y(1, 0, HALF)
+        group_y(1, 0, P)
         quantize_h(2, 1)
-        group_y(1, HALF, BANK)
+        group_y(1, P, BANK)
 
         narrow_beams(3, 0, 0, HALF)
         narrow_beams(3, 1, 0, P, (0, 1, 2))
         bands(2, (0, 1))
         bands(2, (2, 3))
         power(3, 0)
-        quantize_y(1)
-        store_scales(0, CHUNKS[2][0])
+        affine(2, (0, 1))
         quantize_h(3, 0)
-        affine(2)
+        affine(2, (2, 3))
         narrow_beams(3, 1, 0, P, (3,))
         narrow_beams(3, 1, P, HALF)
         power(3, 1, 0, P)
-        group_y(2, 0, P)
+        quantize_y(1)
+        store_scales(0, CHUNKS[2][0])
         quantize_h(3, 1, 0, P)
         power(3, 1, P, HALF)
-        group_y(2, P, HALF)
+        group_y(2, 0, P)
         quantize_h(3, 1, P, HALF)
+        group_y(2, P, HALF)
         turn(1, HALF, BANK)
         turn(2)
         store_rows(1, 2 * P, True)
@@ -504,15 +511,16 @@ def tile_beam_power_log_bands_h2_kernel(
         bands_close(3, ALL, 0, P)
         bands_open(3, ALL, P, HALF)
         bands_close(3, ALL, P, HALF)
-        store_rows(2, P, False)
-        quantize_y(2)
         affine(3, ALL, 0, P)
         turn(3, 0, P)
+        quantize_y(2)
         affine(3, ALL, P, HALF)
         turn(3, P, HALF)
+        store_rows(2, P, True)
         store_rows(3, 0, True)
         group_y(3, 0, P)
         group_y(3, P, HALF)
-        store_rows(3, P, True, nc.scalar)
-        quantize_y(3)
+        quantize_y(3, 0, P)
+        store_rows(3, P, True, (nc.scalar,))
+        quantize_y(3, P, HALF)
         store_scales(CHUNKS[2][0], M)

@@ -380,8 +380,8 @@ def tile_beam_power_log_bands_h2_kernel(
                 )
 
         load_w(RE0, nc.scalar)
-        nc.gpsimd.memset(ws_re[:].bitcast(I32), 0)
-        nc.gpsimd.memset(cal_rows[:].bitcast(I32), 0)
+        zero_plane(ws_re)
+        zero_plane(cal_rows)
         zero_plane(xs_first)
         nc.vector.memset(warm_bf[:].bitcast(F32), 1.0)
         zero_plane(ws_im)
@@ -408,18 +408,18 @@ def tile_beam_power_log_bands_h2_kernel(
         load_band_column(gamma_col, gamma)
         load_band_column(beta_col, beta)
         load_x(2)
-        warm_tensor(14, warm_codes[:])
-        warm_tensor(6, x_codes[0][:, 0, 0:P])
-        deal_cal()
+        warm_tensor(16, warm_codes[:])
         order_w_codes(RE0)
-        turn_cal()
-        root_of_cal()
+        deal_cal()
         order_w_planes(RE0)
+        turn_cal()
+        order_w_planes(RE1)
+        root_of_cal()
         step_of_cal()
         sign_of_cal()
 
         beams(0, 0, 4)
-        order_w(RE1)
+        order_w_codes(RE1)
         beams(0, 8, 12)
         sign_pool(0)
         group_pool(0, 0)
@@ -465,19 +465,20 @@ def tile_beam_power_log_bands_h2_kernel(
         join_blocks(0, BANK)
         store_blocks(0, (0, 1), nc.sync)
         narrow_beams(2, 0, 0, HALF, (2, 3))
+        narrow_beams(2, 1, 0, HALF, (0,))
         bands(1, (0, 1), HALF, BANK)
         bands(1, (2, 3), HALF, BANK)
         store_blocks(0, (2, 3), nc.scalar)
         power(2, 0)
         group_y(0, 0, HALF)
-        narrow_beams(2, 1, 0, HALF, (0, 1))
+        narrow_beams(2, 1, 0, HALF, (1,))
         turn(1, 0, HALF)
         store_rows(1, 0, True)
-        affine(1, ALL, HALF, BANK)
+        store_rows(1, P, True)
         quantize_h(2, 0)
-        narrow_beams(2, 1, 0, HALF, (2, 3))
         group_y(0, HALF, BANK)
-        store_rows(1, P, False)
+        affine(1, ALL, HALF, BANK)
+        narrow_beams(2, 1, 0, HALF, (2, 3))
         quantize_y(0)
         power(2, 1)
         group_y(1, 0, P)

@@ -34,7 +34,7 @@ def tile_beam_power_log_bands_h2_kernel(
         ctx.enter_context(tc.manual_schedule())
 
         def kept(name, shape, dtype):
-            return keep.tile(shape, dtype, name=name, align_bytes=64)
+            return keep.tile(shape, dtype, name=name, align_bytes=256)
 
         def new_bank(shape):
             return psum.tile(shape, F32, name="bank", tag="bank")
@@ -213,8 +213,8 @@ def tile_beam_power_log_bands_h2_kernel(
             m0, m1 = span(c, m0, m1)
             if m0 == 0:
                 width = CHUNKS[c][1]
-                h_codes[(c, g)] = work.tile([P, width], U32, name="h_codes", tag="h_codes", bufs=4, align_bytes=64)
-                h_planes[(c, g)] = work.tile([P, width], U8, name="h_plane", tag="h_plane", bufs=4, align_bytes=64)
+                h_codes[(c, g)] = work.tile([P, width], U32, name="h_codes", tag="h_codes", bufs=4, align_bytes=256)
+                h_planes[(c, g)] = work.tile([P, width], U8, name="h_plane", tag="h_plane", bufs=4, align_bytes=256)
             nc.vector.quantize_mx(
                 out=h_codes[(c, g)][:, m0:m1].bitcast(FP8X4),
                 scales=h_planes[(c, g)][:, m0:m1],

@@ -168,7 +168,7 @@ def tile_beam_power_log_bands_h2_kernel(
         def squares_of(c, g):
             if (c, g) not in squares:
                 squares[(c, g)] = work.tile(
-                    [P, 2, PACK, CHUNKS[c][1]], F32, name="squares", tag="squares", bufs=3, align_bytes=64
+                    [P, 2, PACK, CHUNKS[c][1]], F32, name="squares", tag="squares", bufs=3, align_bytes=256
                 )
             return squares[(c, g)]
 
@@ -200,7 +200,7 @@ def tile_beam_power_log_bands_h2_kernel(
             m0, m1 = span(c, m0, m1)
             if m0 == 0:
                 h_bf[(c, g)] = work.tile(
-                    [P, CHUNKS[c][1] * PACK], BF16, name="h_bf", tag="h_bf", bufs=2, align_bytes=64
+                    [P, CHUNKS[c][1] * PACK], BF16, name="h_bf", tag="h_bf", bufs=2, align_bytes=256
                 )
             nc.vector.tensor_tensor(
                 out=h_bf[(c, g)][:, PACK * m0 : PACK * m1].rearrange("p (c i t) -> p c t i", i=4, t=PACK),
@@ -258,7 +258,7 @@ def tile_beam_power_log_bands_h2_kernel(
 
         def take_log(c, u, m0, m1, src):
             if c not in logs:
-                logs[c] = work.tile([P, PACK, CHUNKS[c][1]], F32, name="logs", tag="logs", bufs=2, align_bytes=64)
+                logs[c] = work.tile([P, PACK, CHUNKS[c][1]], F32, name="logs", tag="logs", bufs=2, align_bytes=256)
             nc.scalar.activation(out=logs[c][:, u, m0:m1], in_=src, func=ACT.Ln, bias=base_col[:, u : u + 1])
 
         def bands(c, slots, m0=0, m1=None):
@@ -284,7 +284,7 @@ def tile_beam_power_log_bands_h2_kernel(
         def affine(c, slots=range(PACK), m0=0, m1=None):
             m0, m1 = span(c, m0, m1)
             if c not in ys:
-                ys[c] = work.tile([P, PACK, CHUNKS[c][1]], F32, name="ys", tag="ys", bufs=3, align_bytes=64)
+                ys[c] = work.tile([P, PACK, CHUNKS[c][1]], F32, name="ys", tag="ys", bufs=3, align_bytes=256)
             for u in slots:
                 nc.vector.tensor_scalar(
                     out=ys[c][:, u, m0:m1],
@@ -298,7 +298,7 @@ def tile_beam_power_log_bands_h2_kernel(
         def group_y(c, m0=0, m1=None):
             m0, m1 = span(c, m0, m1)
             if m0 == 0:
-                y_bf[c] = work.tile([P, CHUNKS[c][1] * PACK], BF16, name="y_bf", tag="y_bf", bufs=2, align_bytes=64)
+                y_bf[c] = work.tile([P, CHUNKS[c][1] * PACK], BF16, name="y_bf", tag="y_bf", bufs=2, align_bytes=256)
             nc.vector.tensor_copy(
                 out=y_bf[c][:, PACK * m0 : PACK * m1].rearrange("p (c i u) -> p c u i", i=4, u=PACK),
                 in_=ys[c][:, :, m0:m1].rearrange("p u (c i) -> p c u i", i=4),
@@ -333,7 +333,7 @@ def tile_beam_power_log_bands_h2_kernel(
                     nc.tensor.transpose(turned[(c, row0)][:, u, :], ys[c][:, u, row0 : row0 + P], ident[:])
 
         def store_rows(c, row0, on_scalar, queues=(nc.sync,)):
-            rows = work.tile([P, N], F32, name="rows", tag="rows", bufs=6, align_bytes=64)
+            rows = work.tile([P, N], F32, name="rows", tag="rows", bufs=6, align_bytes=256)
             first = CHUNKS[c][0] + row0
             share = P // len(queues)
             for i, queue in enumerate(queues):

@@ -423,17 +423,19 @@ def tile_beam_power_log_bands_h2_kernel(
         beams(0, 8, 12)
         sign_pool(0)
         group_pool(0, 0)
-        order_w(IM0)
+        order_w_planes(IM0)
+        order_w_codes(IM0)
         beams(0, 4, 8)
         group_pool(0, 1)
-        order_w(IM1)
+        order_w_planes(IM1)
         sign_pool(1)
+        order_w_codes(IM1)
         beams(0, 12, 16)
         quantize_pool(0)
         group_pool(1, 0)
         group_pool(1, 1)
-        power(0, 0)
         quantize_pool(1)
+        power(0, 0)
         power(0, 1)
         quantize_h(0, 0)
         quantize_h(0, 1)

@@ -429,9 +429,9 @@ def tile_beam_power_log_bands_h2_kernel(
         group_pool(0, 1)
         order_w_planes(IM1)
         sign_pool(1)
+        quantize_pool(0)
         order_w_codes(IM1)
         beams(0, 12, 16)
-        quantize_pool(0)
         group_pool(1, 0)
         group_pool(1, 1)
         quantize_pool(1)

@@ -346,24 +346,33 @@ def tile_beam_power_log_bands_h2_kernel(
                     nc.vector.tensor_copy(out=dst, in_=src)
                 queue.dma_start(out=out_0[first : first + P, cols], in_=rows[:, cols])
 
-        y_blocks = kept("y_blocks", [P, PACK, BANK], F32)
-        y_rows = kept("y_rows", [P, BANK * PACK], F32)
+        y_blocks, y_rows = {}, {}
 
-        def turn_blocks(c, u):
-            nc.vector.transpose(out=y_blocks[:, u, :], in_=ys[c][:, u, :])
+        def turn_blocks(c, u, m0=0, m1=None):
+            m0, m1 = span(c, m0, m1)
+            if (c, m0) not in y_blocks:
+                y_blocks[(c, m0)] = work.tile(
+                    [P, PACK, m1 - m0], F32, name="y_blocks", tag="y_blocks", bufs=1, align_bytes=256
+                )
+            nc.vector.transpose(out=y_blocks[(c, m0)][:, u, :], in_=ys[c][:, u, m0:m1])
 
-        def join_blocks(m0, m1):
+        def join_blocks(c, m0=0, m1=None):
+            m0, m1 = span(c, m0, m1)
+            y_rows[(c, m0)] = work.tile(
+                [P, (m1 - m0) * PACK], F32, name="y_rows", tag="y_rows", bufs=1, align_bytes=256
+            )
             nc.vector.tensor_copy(
-                out=y_rows[:, PACK * m0 : PACK * m1].rearrange("p (c i u) -> p c u i", i=2, u=PACK),
-                in_=y_blocks[:, :, m0:m1].rearrange("p u (c i) -> p c u i", i=2),
+                out=y_rows[(c, m0)][:].rearrange("p (c i u) -> p c u i", i=2, u=PACK),
+                in_=y_blocks[(c, m0)][:].rearrange("p u (c i) -> p c u i", i=2),
             )
 
-        def store_blocks(c, quads, queue):
+        def store_blocks(c, quads, queue, m0=0, m1=None):
+            m0, m1 = span(c, m0, m1)
             first = CHUNKS[c][0]
             for quad in quads:
                 queue.dma_start(
-                    out=out_0[first : first + BANK, P * quad : P * (quad + 1)].rearrange("(j i) n -> i j n", i=32),
-                    in_=y_rows[32 * quad : 32 * (quad + 1), :].rearrange("i (j n) -> i j n", n=P),
+                    out=out_0[first + m0 : first + m1, P * quad : P * (quad + 1)].rearrange("(j i) n -> i j n", i=32),
+                    in_=y_rows[(c, m0)][32 * quad : 32 * (quad + 1), :].rearrange("i (j n) -> i j n", n=P),
                 )
 
         def warm_tensor(passes, moving):
@@ -442,51 +451,54 @@ def tile_beam_power_log_bands_h2_kernel(
 
         HALF = 2 * P
         ALL = tuple(range(PACK))
-        beams(1, 0, 8)
-        power(1, 0)
+        narrow_beams(1, 0, 0, HALF)
+        power(1, 0, 0, HALF)
+        narrow_beams(1, 0, HALF, BANK)
+        power(1, 0, HALF, BANK)
         narrow_beams(1, 1, 0, HALF, (0,))
         for u in range(PACK):
             bands(0, (u,))
-        affine(0)
-        quantize_h(1, 0)
-        narrow_beams(1, 1, 0, HALF, (1, 2, 3))
+        quantize_h(1, 0, 0, HALF)
+        affine(0, (0, 1))
+        quantize_h(1, 0, HALF, BANK)
+        affine(0, (2,))
         turn_blocks(0, 0)
-        power(1, 1, 0, HALF)
+        affine(0, (3,))
+        narrow_beams(1, 1, 0, HALF, (1, 2, 3))
         turn_blocks(0, 1)
+        turn_blocks(0, 2)
+        power(1, 1, 0, HALF)
+        turn_blocks(0, 3)
         quantize_h(1, 1, 0, HALF)
         narrow_beams(1, 1, HALF, BANK)
-        turn_blocks(0, 2)
+        join_blocks(0)
+        store_blocks(0, (0, 1), nc.sync)
         power(1, 1, HALF, BANK)
-        turn_blocks(0, 3)
+        group_y(0, 0, P)
         quantize_h(1, 1, HALF, BANK)
-
         narrow_beams(2, 0, 0, HALF, (0, 1))
         bands(1, (0, 1), 0, HALF)
+        store_blocks(0, (2, 3), nc.scalar)
         bands(1, (2, 3), 0, HALF)
+        group_y(0, P, BANK)
         affine(1, ALL, 0, HALF)
-        join_blocks(0, BANK)
-        store_blocks(0, (0, 1), nc.sync)
         narrow_beams(2, 0, 0, HALF, (2, 3))
         narrow_beams(2, 1, 0, HALF, (0,))
         bands(1, (0, 1), HALF, BANK)
         bands(1, (2, 3), HALF, BANK)
-        store_blocks(0, (2, 3), nc.scalar)
+        quantize_y(0)
         power(2, 0)
-        group_y(0, 0, HALF)
         narrow_beams(2, 1, 0, HALF, (1,))
         turn(1, 0, HALF)
-        store_rows(1, 0, True)
-        store_rows(1, P, True)
-        quantize_h(2, 0)
-        group_y(0, HALF, BANK)
         affine(1, ALL, HALF, BANK)
+        quantize_h(2, 0)
+        store_rows(1, 0, False)
+        store_rows(1, P, False)
         narrow_beams(2, 1, 0, HALF, (2, 3))
-        quantize_y(0)
         power(2, 1)
         group_y(1, 0, P)
         quantize_h(2, 1)
         group_y(1, P, BANK)
-
         narrow_beams(3, 0, 0, HALF)
         narrow_beams(3, 1, 0, P, (0, 1, 2))
         bands(2, (0, 1))

@@ -20,7 +20,7 @@ P = 128
 PACK = 4
 BANK = 512
 RE0, RE1, IM0, IM1 = 0, 1, 2, 3
-CHUNKS = ((0, 512), (512, 512), (1024, 256), (1280, 256))
+CHUNKS = ((0, 512), (512, 512), (1024, 512))
 
 
 def tile_beam_power_log_bands_h2_kernel(
@@ -312,9 +312,11 @@ def tile_beam_power_log_bands_h2_kernel(
                 scales=y_plane[:, first + m0 : first + m1],
                 in_=y_bf[c][:, PACK * m0 : PACK * m1],
             )
-            if m1 == CHUNKS[c][1]:
-                dst = out_1[0].rearrange("p m t -> p (m t)")[:, PACK * first : PACK * (first + m1)]
-                nc.sync.dma_start(out=dst.bitcast(I32), in_=y_codes[c][:].bitcast(I32))
+
+        def store_codes(c, m0=0, m1=BANK):
+            first = CHUNKS[c][0]
+            dst = out_1[0].rearrange("p m t -> p (m t)")[:, PACK * (first + m0) : PACK * (first + m1)]
+            nc.sync.dma_start(out=dst.bitcast(I32), in_=y_codes[c][:, m0:m1].bitcast(I32))
 
         def store_scales(col0, col1, queues=(nc.sync,) * 4):
             for quad in range(4):
@@ -333,7 +335,7 @@ def tile_beam_power_log_bands_h2_kernel(
                     nc.tensor.transpose(turned[(c, row0)][:, u, :], ys[c][:, u, row0 : row0 + P], ident[:])
 
         def store_rows(c, row0, on_scalar, queues=(nc.sync,)):
-            rows = work.tile([P, N], F32, name="rows", tag="rows", bufs=6, align_bytes=256)
+            rows = work.tile([P, N], F32, name="rows", tag="rows", bufs=8, align_bytes=256)
             first = CHUNKS[c][0] + row0
             share = P // len(queues)
             for i, queue in enumerate(queues):
@@ -450,12 +452,13 @@ def tile_beam_power_log_bands_h2_kernel(
         quantize_h(0, 1)
 
         HALF = 2 * P
+        LAST = 3 * P
         ALL = tuple(range(PACK))
         narrow_beams(1, 0, 0, HALF)
         power(1, 0, 0, HALF)
         narrow_beams(1, 0, HALF, BANK)
         power(1, 0, HALF, BANK)
-        narrow_beams(1, 1, 0, HALF, (0,))
+        beams(1, 8, 9)
         for u in range(PACK):
             bands(0, (u,))
         quantize_h(1, 0, 0, HALF)
@@ -464,78 +467,77 @@ def tile_beam_power_log_bands_h2_kernel(
         affine(0, (2,))
         turn_blocks(0, 0)
         affine(0, (3,))
-        narrow_beams(1, 1, 0, HALF, (1, 2, 3))
+        beams(1, 9, 16)
         turn_blocks(0, 1)
         turn_blocks(0, 2)
-        power(1, 1, 0, HALF)
         turn_blocks(0, 3)
-        quantize_h(1, 1, 0, HALF)
-        narrow_beams(1, 1, HALF, BANK)
+        group_y(0, 0, P)
         join_blocks(0)
         store_blocks(0, (0, 1), nc.sync)
-        power(1, 1, HALF, BANK)
-        group_y(0, 0, P)
-        quantize_h(1, 1, HALF, BANK)
-        narrow_beams(2, 0, 0, HALF, (0, 1))
-        bands(1, (0, 1), 0, HALF)
+        power(1, 1)
+        beams(2, 0, 3)
         store_blocks(0, (2, 3), nc.scalar)
-        bands(1, (2, 3), 0, HALF)
-        group_y(0, P, BANK)
-        affine(1, ALL, 0, HALF)
-        narrow_beams(2, 0, 0, HALF, (2, 3))
+        beams(2, 3, 8)
+        group_y(0, P, HALF)
+        quantize_h(1, 1)
+        group_y(0, HALF, BANK)
         narrow_beams(2, 1, 0, HALF, (0,))
-        bands(1, (0, 1), HALF, BANK)
-        bands(1, (2, 3), HALF, BANK)
+        bands(1, (0,))
+        bands(1, (1,))
+        bands(1, (2,))
+        bands(1, (3,))
         quantize_y(0)
+        store_codes(0)
+        store_scales(0, BANK)
         power(2, 0)
-        narrow_beams(2, 1, 0, HALF, (1,))
-        turn(1, 0, HALF)
-        affine(1, ALL, HALF, BANK)
+        affine(1)
         quantize_h(2, 0)
-        store_rows(1, 0, False)
-        store_rows(1, P, False)
-        narrow_beams(2, 1, 0, HALF, (2, 3))
-        power(2, 1)
+        narrow_beams(2, 1, 0, HALF, (1, 2, 3))
         group_y(1, 0, P)
-        quantize_h(2, 1)
-        group_y(1, P, BANK)
-        narrow_beams(3, 0, 0, HALF)
-        narrow_beams(3, 1, 0, P, (0, 1, 2))
-        bands(2, (0, 1))
-        bands(2, (2, 3))
-        power(3, 0)
-        affine(2, (0, 1))
-        quantize_h(3, 0)
-        affine(2, (2, 3))
-        narrow_beams(3, 1, 0, P, (3,))
-        narrow_beams(3, 1, P, HALF)
-        power(3, 1, 0, P)
+        power(2, 1, 0, HALF)
+        narrow_beams(2, 1, HALF, LAST, (0, 1))
+        turn(1, 0, LAST)
+        store_rows(1, 0, True)
+        store_rows(1, P, True)
+        narrow_beams(2, 1, HALF, LAST, (2, 3))
+        group_y(1, P, HALF)
+        quantize_h(2, 1, 0, HALF)
+        group_y(1, HALF, BANK)
+        narrow_beams(2, 1, LAST, BANK, (0, 1))
+        bands(2, (0, 1), 0, HALF)
+        narrow_beams(2, 1, LAST, BANK, (2, 3))
+        bands(2, (2, 3), 0, HALF)
+        power(2, 1, HALF, LAST)
         quantize_y(1)
-        store_scales(0, CHUNKS[2][0])
-        quantize_h(3, 1, 0, P)
-        power(3, 1, P, HALF)
-        group_y(2, 0, P)
-        quantize_h(3, 1, P, HALF)
-        group_y(2, P, HALF)
-        turn(1, HALF, BANK)
-        turn(2)
-        store_rows(1, 2 * P, True)
-        store_rows(1, 3 * P, True)
+        store_codes(1)
+        quantize_h(2, 1, HALF, LAST)
+        store_rows(1, HALF, False)
+        affine(2, (0, 1), 0, HALF)
+        power(2, 1, LAST, BANK)
+        affine(2, (2, 3), 0, HALF)
+        quantize_h(2, 1, LAST, BANK)
+        turn(1, LAST, BANK)
+        store_rows(1, LAST, True)
+        bands_open(2, ALL, HALF, LAST)
+        bands_close(2, ALL, HALF, LAST)
+        bands_open(2, ALL, LAST, BANK)
+        turn(2, 0, P)
         store_rows(2, 0, True)
-        bands_open(3, ALL, 0, P)
-        bands_close(3, ALL, 0, P)
-        bands_open(3, ALL, P, HALF)
-        bands_close(3, ALL, P, HALF)
-        affine(3, ALL, 0, P)
-        turn(3, 0, P)
-        quantize_y(2)
-        affine(3, ALL, P, HALF)
-        turn(3, P, HALF)
+        bands_close(2, ALL, LAST, BANK)
+        turn(2, P, HALF)
+        group_y(2, 0, HALF)
+        affine(2, ALL, HALF, LAST)
+        turn(2, HALF, LAST)
+        quantize_y(2, 0, HALF)
+        store_codes(2, 0, HALF)
+        group_y(2, HALF, LAST)
+        affine(2, ALL, LAST, BANK)
+        turn(2, LAST, BANK)
         store_rows(2, P, True)
-        store_rows(3, 0, True)
-        group_y(3, 0, P)
-        group_y(3, P, HALF)
-        quantize_y(3, 0, P)
-        store_rows(3, P, True, (nc.scalar,))
-        quantize_y(3, P, HALF)
-        store_scales(CHUNKS[2][0], M)
+        quantize_y(2, HALF, LAST)
+        group_y(2, LAST, BANK)
+        store_rows(2, HALF, True)
+        quantize_y(2, LAST, BANK)
+        store_codes(2, HALF, BANK)
+        store_rows(2, LAST, True, (nc.scalar,))
+        store_scales(BANK, M)

@@ -61,7 +61,9 @@ def tile_beam_power_log_bands_h2_kernel(
         cal_sign = kept("cal_sign", [P, 2 * PACK], F32)
         w_raw = [kept("w_raw%d" % q, [P, 2, 2 * BANK], U8) for q in range(4)]
         w_codes = [kept("w_codes%d" % q, [P, 2, 2 * BANK], U8) for q in range(4)]
-        w_planes = [kept("w_planes%d" % q, [P, 2, BANK], U8) for q in range(4)]
+        im_planes = kept("im_planes", [P, 2, F], U8)
+        w_planes = [kept("w_planes%d" % q, [P, 2, BANK], U8) for q in (RE0, RE1)]
+        w_planes.extend((im_planes[:, :, 0:BANK], im_planes[:, :, BANK:F]))
         x_codes = [kept("x_codes%d" % i, [P, 2, BANK], U32) for i in range(3)]
         pool_raw = [kept("pool_raw%d" % g, [P, PACK, N], BF16) for g in range(2)]
         pool_grouped = [kept("pool_grouped%d" % g, [P, N * PACK], BF16) for g in range(2)]
@@ -133,6 +135,12 @@ def tile_beam_power_log_bands_h2_kernel(
             nc.vector.tensor_copy(
                 out=w_planes[q][:].bitcast(I32).rearrange("p g (t b w) -> p g t b w", t=PACK, w=2),
                 in_=raw_plane.bitcast(I32).rearrange("p g (b t w) -> p g t b w", t=PACK, w=2),
+            )
+
+        def order_im_planes():
+            nc.vector.tensor_copy(
+                out=im_planes[:].bitcast(I32).rearrange("p g (h t b w) -> p (g h) t b w", h=2, t=PACK, w=2),
+                in_=ws_im[:].bitcast(I32).rearrange("p g (h b t w) -> p (g h) t b w", h=2, t=PACK, w=2),
             )
 
         def order_w_codes(q):
@@ -231,8 +239,8 @@ def tile_beam_power_log_bands_h2_kernel(
                     op0=ALU.mult,
                 )
 
-        def group_pool(g, part):
-            pairs = slice(32 * part, 32 * (part + 1))
+        def group_pool(g, part0, part1):
+            pairs = slice(32 * part0, 32 * part1)
             nc.vector.tensor_copy(
                 out=pool_grouped[g][:].rearrange("p (u c i t) -> p c t i u", u=PACK, i=2, t=PACK)[:, pairs],
                 in_=pool_raw[g][:].rearrange("p t (c i u) -> p c t i u", i=2, u=PACK)[:, pairs],
@@ -354,14 +362,14 @@ def tile_beam_power_log_bands_h2_kernel(
             m0, m1 = span(c, m0, m1)
             if (c, m0) not in y_blocks:
                 y_blocks[(c, m0)] = work.tile(
-                    [P, PACK, m1 - m0], F32, name="y_blocks", tag="y_blocks", bufs=1, align_bytes=256
+                    [P, PACK, m1 - m0], F32, name="y_blocks", tag="y_blocks%d" % c, bufs=1, align_bytes=256
                 )
             nc.vector.transpose(out=y_blocks[(c, m0)][:, u, :], in_=ys[c][:, u, m0:m1])
 
         def join_blocks(c, m0=0, m1=None):
             m0, m1 = span(c, m0, m1)
             y_rows[(c, m0)] = work.tile(
-                [P, (m1 - m0) * PACK], F32, name="y_rows", tag="y_rows", bufs=1, align_bytes=256
+                [P, (m1 - m0) * PACK], F32, name="y_rows", tag="y_rows%d" % c, bufs=1, align_bytes=256
             )
             nc.vector.tensor_copy(
                 out=y_rows[(c, m0)][:].rearrange("p (c i u) -> p c u i", i=2, u=PACK),
@@ -433,18 +441,16 @@ def tile_beam_power_log_bands_h2_kernel(
         order_w_codes(RE1)
         beams(0, 8, 12)
         sign_pool(0)
-        group_pool(0, 0)
-        order_w_planes(IM0)
+        group_pool(0, 0, 1)
+        order_im_planes()
         order_w_codes(IM0)
         beams(0, 4, 8)
-        group_pool(0, 1)
-        order_w_planes(IM1)
+        group_pool(0, 1, 2)
         sign_pool(1)
         quantize_pool(0)
         order_w_codes(IM1)
         beams(0, 12, 16)
-        group_pool(1, 0)
-        group_pool(1, 1)
+        group_pool(1, 0, 2)
         quantize_pool(1)
         power(0, 0)
         power(0, 1)
@@ -461,27 +467,23 @@ def tile_beam_power_log_bands_h2_kernel(
         beams(1, 8, 9)
         for u in range(PACK):
             bands(0, (u,))
-        quantize_h(1, 0, 0, HALF)
-        affine(0, (0, 1))
-        quantize_h(1, 0, HALF, BANK)
-        affine(0, (2,))
+        affine(0, (0,))
+        quantize_h(1, 0)
+        affine(0, (1, 2))
         turn_blocks(0, 0)
         affine(0, (3,))
         beams(1, 9, 16)
         turn_blocks(0, 1)
         turn_blocks(0, 2)
         turn_blocks(0, 3)
-        group_y(0, 0, P)
+        group_y(0, 0, LAST)
         join_blocks(0)
-        store_blocks(0, (0, 1), nc.sync)
+        store_blocks(0, (0, 2, 1, 3), nc.sync)
         power(1, 1)
-        beams(2, 0, 3)
-        store_blocks(0, (2, 3), nc.scalar)
-        beams(2, 3, 8)
-        group_y(0, P, HALF)
+        beams(2, 0, 8)
+        group_y(0, LAST, BANK)
         quantize_h(1, 1)
-        group_y(0, HALF, BANK)
-        narrow_beams(2, 1, 0, HALF, (0,))
+        narrow_beams(2, 1, 0, HALF, (0, 1))
         bands(1, (0,))
         bands(1, (1,))
         bands(1, (2,))
@@ -492,13 +494,14 @@ def tile_beam_power_log_bands_h2_kernel(
         power(2, 0)
         affine(1)
         quantize_h(2, 0)
-        narrow_beams(2, 1, 0, HALF, (1, 2, 3))
+        narrow_beams(2, 1, 0, HALF, (2, 3))
         group_y(1, 0, P)
         power(2, 1, 0, HALF)
         narrow_beams(2, 1, HALF, LAST, (0, 1))
         turn(1, 0, LAST)
         store_rows(1, 0, True)
         store_rows(1, P, True)
+        store_rows(1, HALF, True)
         narrow_beams(2, 1, HALF, LAST, (2, 3))
         group_y(1, P, HALF)
         quantize_h(2, 1, 0, HALF)
@@ -511,7 +514,6 @@ def tile_beam_power_log_bands_h2_kernel(
         quantize_y(1)
         store_codes(1)
         quantize_h(2, 1, HALF, LAST)
-        store_rows(1, HALF, False)
         affine(2, (0, 1), 0, HALF)
         power(2, 1, LAST, BANK)
         affine(2, (2, 3), 0, HALF)
@@ -530,14 +532,14 @@ def tile_beam_power_log_bands_h2_kernel(
         turn(2, HALF, LAST)
         quantize_y(2, 0, HALF)
         store_codes(2, 0, HALF)
-        group_y(2, HALF, LAST)
         affine(2, ALL, LAST, BANK)
         turn(2, LAST, BANK)
         store_rows(2, P, True)
-        quantize_y(2, HALF, LAST)
+        group_y(2, HALF, LAST)
         group_y(2, LAST, BANK)
         store_rows(2, HALF, True)
+        quantize_y(2, HALF, LAST)
         quantize_y(2, LAST, BANK)
         store_codes(2, HALF, BANK)
-        store_rows(2, LAST, True, (nc.scalar,))
+        store_rows(2, LAST, True)
         store_scales(BANK, M)

@@ -478,9 +478,11 @@ def tile_beam_power_log_bands_h2_kernel(
         turn_blocks(0, 3)
         group_y(0, 0, LAST)
         join_blocks(0)
-        store_blocks(0, (0, 2, 1, 3), nc.sync)
+        store_blocks(0, (0, 1), nc.sync)
         power(1, 1)
-        beams(2, 0, 8)
+        beams(2, 0, 3)
+        store_blocks(0, (2, 3), nc.scalar)
+        beams(2, 3, 8)
         group_y(0, LAST, BANK)
         quantize_h(1, 1)
         narrow_beams(2, 1, 0, HALF, (0, 1))
@@ -540,6 +542,6 @@ def tile_beam_power_log_bands_h2_kernel(
         store_rows(2, HALF, True)
         quantize_y(2, HALF, LAST)
         quantize_y(2, LAST, BANK)
+        store_rows(2, LAST, True, (nc.scalar,))
         store_codes(2, HALF, BANK)
-        store_rows(2, LAST, True)
         store_scales(BANK, M)

@@ -239,16 +239,17 @@ def tile_beam_power_log_bands_h2_kernel(
                     op0=ALU.mult,
                 )
 
-        def group_pool(g, part0, part1):
-            pairs = slice(32 * part0, 32 * part1)
+        def group_pool(g, u0, u1):
             nc.vector.tensor_copy(
-                out=pool_grouped[g][:].rearrange("p (u c i t) -> p c t i u", u=PACK, i=2, t=PACK)[:, pairs],
-                in_=pool_raw[g][:].rearrange("p t (c i u) -> p c t i u", i=2, u=PACK)[:, pairs],
+                out=pool_grouped[g][:].rearrange("p (u c i t) -> p c t i u", u=PACK, i=2, t=PACK)[:, :, :, :, u0:u1],
+                in_=pool_raw[g][:].rearrange("p t (c i u) -> p c t i u", i=2, u=PACK)[:, :, :, :, u0:u1],
             )
 
-        def quantize_pool(g):
+        def quantize_pool(g, u0=0, u1=PACK):
             nc.vector.quantize_mx(
-                out=pool_codes[g][:].bitcast(FP8X4), scales=pool_planes[g][:], in_=pool_grouped[g][:]
+                out=pool_codes[g][:, P * u0 : P * u1].bitcast(FP8X4),
+                scales=pool_planes[g][:, P * u0 : P * u1],
+                in_=pool_grouped[g][:, N * u0 : N * u1],
             )
 
         logs, ys, y_bf, energy = {}, {}, {}, {}
@@ -358,13 +359,13 @@ def tile_beam_power_log_bands_h2_kernel(
 
         y_blocks, y_rows = {}, {}
 
-        def turn_blocks(c, u, m0=0, m1=None):
-            m0, m1 = span(c, m0, m1)
-            if (c, m0) not in y_blocks:
-                y_blocks[(c, m0)] = work.tile(
-                    [P, PACK, m1 - m0], F32, name="y_blocks", tag="y_blocks%d" % c, bufs=1, align_bytes=256
-                )
-            nc.vector.transpose(out=y_blocks[(c, m0)][:, u, :], in_=ys[c][:, u, m0:m1])
+        def turn_blocks(c, u0, u1):
+            if (c, 0) not in y_blocks:
+                y_blocks[(c, 0)] = kept("y_blocks", [P, PACK, BANK], F32)
+            nc.vector.transpose(
+                out=y_blocks[(c, 0)][:, u0:u1, :].rearrange("p u m -> p (u m)"),
+                in_=ys[c][:, u0:u1, :].rearrange("p u m -> p (u m)"),
+            )
 
         def join_blocks(c, m0=0, m1=None):
             m0, m1 = span(c, m0, m1)
@@ -441,17 +442,19 @@ def tile_beam_power_log_bands_h2_kernel(
         order_w_codes(RE1)
         beams(0, 8, 12)
         sign_pool(0)
-        group_pool(0, 0, 1)
+        group_pool(0, 0, 2)
         order_im_planes()
         order_w_codes(IM0)
         beams(0, 4, 8)
-        group_pool(0, 1, 2)
+        group_pool(0, 2, 4)
         sign_pool(1)
         quantize_pool(0)
         order_w_codes(IM1)
         beams(0, 12, 16)
         group_pool(1, 0, 2)
-        quantize_pool(1)
+        group_pool(1, 2, 4)
+        quantize_pool(1, 0, 2)
+        quantize_pool(1, 2, 4)
         power(0, 0)
         power(0, 1)
         quantize_h(0, 0)
@@ -469,20 +472,17 @@ def tile_beam_power_log_bands_h2_kernel(
             bands(0, (u,))
         affine(0, (0,))
         quantize_h(1, 0)
-        affine(0, (1, 2))
-        turn_blocks(0, 0)
-        affine(0, (3,))
+        affine(0, (1, 2, 3))
         beams(1, 9, 16)
-        turn_blocks(0, 1)
-        turn_blocks(0, 2)
-        turn_blocks(0, 3)
+        turn_blocks(0, 0, 2)
+        turn_blocks(0, 2, 4)
         group_y(0, 0, LAST)
         join_blocks(0)
         store_blocks(0, (0, 1), nc.sync)
         power(1, 1)
-        beams(2, 0, 3)
+        beams(2, 0, 6)
         store_blocks(0, (2, 3), nc.scalar)
-        beams(2, 3, 8)
+        beams(2, 6, 8)
         group_y(0, LAST, BANK)
         quantize_h(1, 1)
         narrow_beams(2, 1, 0, HALF, (0, 1))

@@ -20,6 +20,7 @@ P = 128
 PACK = 4
 BANK = 512
 RE0, RE1, IM0, IM1 = 0, 1, 2, 3
+TINY = 1e-26
 CHUNKS = ((0, 512), (512, 512), (1024, 512))
 
 
@@ -43,22 +44,21 @@ def tile_beam_power_log_bands_h2_kernel(
         ws_im = kept("ws_im", [P, 2, F], U8)
         xs_first = kept("xs_first", [P, 2, BANK], U8)
         xs_rest = kept("xs_rest", [P, 2, 2 * BANK], U8)
+        one = kept("one", [P, 1], F32)
+        warm_root = kept("warm_root", [P, 1], F32)
         warm_ln = kept("warm_ln", [P, 1], F32)
         warm_bf = kept("warm_bf", [P, PACK * P], BF16)
         warm_codes = kept("warm_codes", [P, P], U32)
         warm_plane = kept("warm_plane", [P, P], U8)
-        half = kept("half", [P, 2 * PACK], F32)
         ident = kept("ident", [P, P], F32)
         base_col = kept("base_col", [P, PACK], BF16)
         gamma_col = kept("gamma_col", [P, PACK], BF16)
         beta_col = kept("beta_col", [P, PACK], BF16)
         cal_rows = kept("cal_rows", [P, 2 * P], BF16)
-        cal_dealt = kept("cal_dealt", [P, 2 * P], BF16)
-        cal_turned = kept("cal_turned", [P, 2 * PACK, 32], BF16)
-        cal_abs = kept("cal_abs", [P, 2 * PACK], F32)
-        cal_root = kept("cal_root", [P, 2 * PACK], F32)
-        cal_step = kept("cal_step", [P, 2 * PACK], F32)
-        cal_sign = kept("cal_sign", [P, 2 * PACK], F32)
+        inv_root = kept("inv_root", [P, 2 * P], F32)
+        root_rows = [kept("root_rows%d" % g, [P, P], F32) for g in range(2)]
+        roots = kept("roots", [P, 2 * PACK, 32], F32)
+        half_sign = kept("half_sign", [P, 2 * PACK], F32)
         w_raw = [kept("w_raw%d" % q, [P, 2, 2 * BANK], U8) for q in range(4)]
         w_codes = [kept("w_codes%d" % q, [P, 2, 2 * BANK], U8) for q in range(4)]
         im_planes = kept("im_planes", [P, 2, F], U8)
@@ -105,30 +105,27 @@ def tile_beam_power_log_bands_h2_kernel(
         def load_band_column(col, vec):
             nc.sync.dma_start(out=col[:], in_=vec.rearrange("(p t) -> p t", t=PACK))
 
-        def deal_cal():
-            nc.vector.tensor_copy(
-                out=cal_dealt[:].rearrange("p (g t b r) -> p g t b r", g=2, t=PACK, r=8),
-                in_=cal_rows[:].rearrange("p (g b t r) -> p g t b r", g=2, t=PACK, r=8),
+        def inverse_root_of_cal():
+            nc.scalar.activation(out=inv_root[:], in_=cal_rows[:], func=ACT.Abs_reciprocal_sqrt, bias=TINY)
+
+        def root_of_cal(g):
+            cols = slice(P * g, P * (g + 1))
+            nc.vector.tensor_tensor(
+                out=root_rows[g][:].rearrange("p (t b r) -> p t b r", t=PACK, r=8),
+                in0=inv_root[:, cols].rearrange("p (b t r) -> p t b r", t=PACK, r=8),
+                in1=cal_rows[:, cols].rearrange("p (b t r) -> p t b r", t=PACK, r=8),
+                op=ALU.mult,
             )
 
-        def turn_cal():
-            nc.vector.transpose(out=cal_turned[:].rearrange("p j c -> p (j c)"), in_=cal_dealt[:])
-
-        def root_of_cal():
-            values = cal_turned[:, :, 0]
-            nc.vector.scalar_tensor_tensor(
-                out=cal_abs[:], in0=values, scalar=-1.0, in1=values, op0=ALU.mult, op1=ALU.max
-            )
-            for cols in (slice(0, 1), slice(1, PACK), slice(PACK, 2 * PACK)):
-                nc.gpsimd.tensor_tensor(out=cal_root[:, cols], in0=cal_abs[:, cols], in1=half[:, cols], op=ALU.pow)
-
-        def step_of_cal():
-            nc.vector.tensor_scalar(
-                out=cal_step[:], in0=cal_turned[:, :, 0], scalar1=0.0, scalar2=2.0, op0=ALU.is_ge, op1=ALU.mult
+        def turn_root(g):
+            nc.vector.transpose(
+                out=roots[:, PACK * g : PACK * (g + 1), :].rearrange("p j c -> p (j c)"), in_=root_rows[g][:]
             )
 
         def sign_of_cal():
-            nc.vector.tensor_scalar(out=cal_sign[:], in0=cal_step[:], scalar1=1.0, scalar2=None, op0=ALU.subtract)
+            nc.vector.tensor_scalar(
+                out=half_sign[:], in0=roots[:, :, 0], scalar1=0.0, scalar2=0.5, op0=ALU.is_ge, op1=ALU.subtract
+            )
 
         def order_w_planes(q):
             raw_plane = (ws_re, ws_im)[q // 2][:, :, BANK * (q % 2) : BANK * (q % 2 + 1)]
@@ -191,7 +188,7 @@ def tile_beam_power_log_bands_h2_kernel(
                 out=squares_of(c, g)[:, parts[0] : parts[-1] + 1, t, m0:m1],
                 in_=bank[:],
                 func=ACT.Square,
-                scale=cal_root[:, PACK * g + t : PACK * g + t + 1],
+                scale=roots[:, PACK * g + t, 0:1],
             )
 
         def beams(c, j0, j1):
@@ -234,9 +231,10 @@ def tile_beam_power_log_bands_h2_kernel(
                 nc.vector.tensor_scalar(
                     out=pool_raw[g][:, t, :],
                     in0=pool_raw[g][:, t, :],
-                    scalar1=cal_sign[:, PACK * g + t : PACK * g + t + 1],
-                    scalar2=None,
+                    scalar1=half_sign[:, PACK * g + t : PACK * g + t + 1],
+                    scalar2=2.0,
                     op0=ALU.mult,
+                    op1=ALU.mult,
                 )
 
         def group_pool(g, u0, u1):
@@ -293,7 +291,7 @@ def tile_beam_power_log_bands_h2_kernel(
         def affine(c, slots=range(PACK), m0=0, m1=None):
             m0, m1 = span(c, m0, m1)
             if c not in ys:
-                ys[c] = work.tile([P, PACK, CHUNKS[c][1]], F32, name="ys", tag="ys", bufs=3, align_bytes=256)
+                ys[c] = work.tile([P, PACK, CHUNKS[c][1]], F32, name="ys", tag="ys", bufs=2, align_bytes=256)
             for u in slots:
                 nc.vector.tensor_scalar(
                     out=ys[c][:, u, m0:m1],
@@ -357,33 +355,59 @@ def tile_beam_power_log_bands_h2_kernel(
                     nc.vector.tensor_copy(out=dst, in_=src)
                 queue.dma_start(out=out_0[first : first + P, cols], in_=rows[:, cols])
 
-        y_blocks, y_rows = {}, {}
+        HALF = 2 * P
+        LAST = 3 * P
+        ALL = tuple(range(PACK))
+        y_halves = kept("y_halves", [P, 2, PACK, HALF], F32)
+        y_blocks = kept("y_blocks", [P, 2, PACK, HALF], F32)
+        y_rows = kept("y_rows", [P, BANK * PACK], F32)
 
-        def turn_blocks(c, u0, u1):
-            if (c, 0) not in y_blocks:
-                y_blocks[(c, 0)] = kept("y_blocks", [P, PACK, BANK], F32)
+        def affine_halves(slots):
+            for u in slots:
+                nc.vector.tensor_scalar(
+                    out=y_halves[:, :, u, :],
+                    in0=logs[0][:, u, :].rearrange("p (h m) -> p h m", h=2),
+                    scalar1=gamma_col[:, u : u + 1],
+                    scalar2=beta_col[:, u : u + 1],
+                    op0=ALU.mult,
+                    op1=ALU.add,
+                )
+
+        def turn_blocks(h):
             nc.vector.transpose(
-                out=y_blocks[(c, 0)][:, u0:u1, :].rearrange("p u m -> p (u m)"),
-                in_=ys[c][:, u0:u1, :].rearrange("p u m -> p (u m)"),
+                out=y_blocks[:, h].rearrange("p u m -> p (u m)"), in_=y_halves[:, h].rearrange("p u m -> p (u m)")
             )
 
-        def join_blocks(c, m0=0, m1=None):
-            m0, m1 = span(c, m0, m1)
-            y_rows[(c, m0)] = work.tile(
-                [P, (m1 - m0) * PACK], F32, name="y_rows", tag="y_rows%d" % c, bufs=1, align_bytes=256
-            )
-            nc.vector.tensor_copy(
-                out=y_rows[(c, m0)][:].rearrange("p (c i u) -> p c u i", i=2, u=PACK),
-                in_=y_blocks[(c, m0)][:].rearrange("p u (c i) -> p c u i", i=2),
-            )
+        def interleave(dst, src, h, m0, m1, run):
+            cols = slice(PACK * (HALF * h + m0), PACK * (HALF * h + m1))
+            if run is None:
+                nc.gpsimd.tensor_scalar(
+                    out=dst[:, cols].rearrange("p (m u) -> p m u", u=PACK),
+                    in0=src[:, h, :, m0:m1].rearrange("p u m -> p m u"),
+                    scalar1=1.0,
+                    scalar2=-0.0,
+                    op0=ALU.mult,
+                    op1=ALU.add,
+                )
+            else:
+                nc.vector.tensor_copy(
+                    out=dst[:, cols].rearrange("p (c i u) -> p c u i", i=run, u=PACK),
+                    in_=src[:, h, :, m0:m1].rearrange("p u (c i) -> p c u i", i=run),
+                )
 
-        def store_blocks(c, quads, queue, m0=0, m1=None):
-            m0, m1 = span(c, m0, m1)
-            first = CHUNKS[c][0]
+        def group_half(h, m0, m1, on_gpsimd=False):
+            if 0 not in y_bf:
+                y_bf[0] = work.tile([P, BANK * PACK], BF16, name="y_bf", tag="y_bf", bufs=2, align_bytes=256)
+            interleave(y_bf[0], y_halves, h, m0, m1, None if on_gpsimd else 4)
+
+        def join_half(h, m0, m1, on_gpsimd=False):
+            interleave(y_rows, y_blocks, h, m0, m1, None if on_gpsimd else 2)
+
+        def store_blocks(quads, queue):
             for quad in quads:
                 queue.dma_start(
-                    out=out_0[first + m0 : first + m1, P * quad : P * (quad + 1)].rearrange("(j i) n -> i j n", i=32),
-                    in_=y_rows[(c, m0)][32 * quad : 32 * (quad + 1), :].rearrange("i (j n) -> i j n", n=P),
+                    out=out_0[0:BANK, P * quad : P * (quad + 1)].rearrange("(j i) n -> i j n", i=32),
+                    in_=y_rows[32 * quad : 32 * (quad + 1), :].rearrange("i (j n) -> i j n", n=P),
                 )
 
         def warm_tensor(passes, moving):
@@ -400,21 +424,22 @@ def tile_beam_power_log_bands_h2_kernel(
                 )
 
         load_w(RE0, nc.scalar)
-        zero_plane(ws_re)
+        nc.gpsimd.memset(one[:], 1.0)
+        nc.scalar.activation(out=warm_root[:], in_=one[:], func=ACT.Abs_reciprocal_sqrt, bias=TINY)
         zero_plane(cal_rows)
+        zero_plane(ws_re)
         zero_plane(xs_first)
         nc.vector.memset(warm_bf[:].bitcast(F32), 1.0)
         zero_plane(ws_im)
         nc.vector.quantize_mx(out=warm_codes[:].bitcast(FP8X4), scales=warm_plane[:], in_=warm_bf[:])
         zero_plane(xs_rest)
         nc.vector.memset(ident[:], 0.0)
-        nc.gpsimd.memset(half[:], 0.5)
         make_identity(nc, ident[:], nomemset=True)
-        load_scales(ws_re, w_scales, 0, F, rows=(0, 1))
         load_cal(nc.sync)
-        load_scales(ws_re, w_scales, 0, F, rows=(2, 3))
+        load_scales(ws_re, w_scales, 0, F)
         load_x(0)
-        nc.scalar.activation(out=warm_ln[:], in_=half[:, 0:1], func=ACT.Ln)
+        inverse_root_of_cal()
+        nc.scalar.activation(out=warm_ln[:], in_=one[:], func=ACT.Ln)
         load_scales(xs_first, x_scales, 0, BANK)
         load_w(RE1)
         load_pool(0)
@@ -430,12 +455,12 @@ def tile_beam_power_log_bands_h2_kernel(
         load_x(2)
         warm_tensor(16, warm_codes[:])
         order_w_codes(RE0)
-        deal_cal()
         order_w_planes(RE0)
-        turn_cal()
+        root_of_cal(0)
+        root_of_cal(1)
+        turn_root(0)
+        turn_root(1)
         order_w_planes(RE1)
-        root_of_cal()
-        step_of_cal()
         sign_of_cal()
 
         beams(0, 0, 4)
@@ -460,86 +485,81 @@ def tile_beam_power_log_bands_h2_kernel(
         quantize_h(0, 0)
         quantize_h(0, 1)
 
-        HALF = 2 * P
-        LAST = 3 * P
-        ALL = tuple(range(PACK))
+        SHARE = 192
         narrow_beams(1, 0, 0, HALF)
         power(1, 0, 0, HALF)
         narrow_beams(1, 0, HALF, BANK)
         power(1, 0, HALF, BANK)
-        beams(1, 8, 9)
         for u in range(PACK):
             bands(0, (u,))
-        affine(0, (0,))
+        affine_halves((0,))
         quantize_h(1, 0)
-        affine(0, (1, 2, 3))
-        beams(1, 9, 16)
-        turn_blocks(0, 0, 2)
-        turn_blocks(0, 2, 4)
-        group_y(0, 0, LAST)
-        join_blocks(0)
-        store_blocks(0, (0, 1), nc.sync)
+        affine_halves((1, 2, 3))
+        beams(1, 8, 16)
+        group_half(0, 0, SHARE, True)
+        turn_blocks(0)
+        join_half(0, 0, SHARE, True)
+        turn_blocks(1)
+        join_half(0, SHARE, HALF)
+        join_half(1, 0, P)
         power(1, 1)
-        beams(2, 0, 6)
-        store_blocks(0, (2, 3), nc.scalar)
-        beams(2, 6, 8)
-        group_y(0, LAST, BANK)
+        join_half(1, P, HALF)
+        store_blocks((0, 1), nc.sync)
         quantize_h(1, 1)
-        narrow_beams(2, 1, 0, HALF, (0, 1))
-        bands(1, (0,))
-        bands(1, (1,))
-        bands(1, (2,))
-        bands(1, (3,))
+        beams(2, 0, 6)
+        store_blocks((2, 3), nc.scalar)
+        beams(2, 6, 8)
+        group_half(0, SHARE, HALF)
+        group_half(1, 0, HALF)
+        narrow_beams(2, 1, 0, HALF, (0,))
+        for u in range(PACK):
+            bands(1, (u,))
         quantize_y(0)
         store_codes(0)
         store_scales(0, BANK)
         power(2, 0)
-        affine(1)
+        affine(1, (0, 1, 2, 3))
         quantize_h(2, 0)
-        narrow_beams(2, 1, 0, HALF, (2, 3))
-        group_y(1, 0, P)
+        narrow_beams(2, 1, 0, HALF, (1, 2, 3))
+        narrow_beams(2, 1, HALF, LAST)
+        group_y(1, 0, HALF)
         power(2, 1, 0, HALF)
-        narrow_beams(2, 1, HALF, LAST, (0, 1))
-        turn(1, 0, LAST)
-        store_rows(1, 0, True)
-        store_rows(1, P, True)
-        store_rows(1, HALF, True)
-        narrow_beams(2, 1, HALF, LAST, (2, 3))
-        group_y(1, P, HALF)
+        turn(1, 0, HALF)
+        narrow_beams(2, 1, LAST, BANK)
+        store_rows(1, 0, False)
         quantize_h(2, 1, 0, HALF)
-        group_y(1, HALF, BANK)
-        narrow_beams(2, 1, LAST, BANK, (0, 1))
-        bands(2, (0, 1), 0, HALF)
-        narrow_beams(2, 1, LAST, BANK, (2, 3))
-        bands(2, (2, 3), 0, HALF)
         power(2, 1, HALF, LAST)
-        quantize_y(1)
-        store_codes(1)
-        quantize_h(2, 1, HALF, LAST)
-        affine(2, (0, 1), 0, HALF)
-        power(2, 1, LAST, BANK)
-        affine(2, (2, 3), 0, HALF)
-        quantize_h(2, 1, LAST, BANK)
-        turn(1, LAST, BANK)
+        turn(1, HALF, BANK)
+        store_rows(1, P, False)
+        store_rows(1, HALF, True)
         store_rows(1, LAST, True)
+        quantize_h(2, 1, HALF, LAST)
+        bands(2, (0, 1), 0, HALF)
+        bands(2, (2, 3), 0, HALF)
+        power(2, 1, LAST, BANK)
+        group_y(1, HALF, LAST)
+        quantize_h(2, 1, LAST, BANK)
         bands_open(2, ALL, HALF, LAST)
         bands_close(2, ALL, HALF, LAST)
         bands_open(2, ALL, LAST, BANK)
-        turn(2, 0, P)
-        store_rows(2, 0, True)
         bands_close(2, ALL, LAST, BANK)
-        turn(2, P, HALF)
-        group_y(2, 0, HALF)
+        group_y(1, LAST, BANK)
+        affine(2, ALL, 0, HALF)
+        turn(2, 0, HALF)
+        quantize_y(1)
+        store_codes(1)
         affine(2, ALL, HALF, LAST)
-        turn(2, HALF, LAST)
-        quantize_y(2, 0, HALF)
-        store_codes(2, 0, HALF)
+        store_rows(2, 0, True)
+        group_y(2, 0, P)
         affine(2, ALL, LAST, BANK)
-        turn(2, LAST, BANK)
+        turn(2, HALF, BANK)
+        group_y(2, P, HALF)
         store_rows(2, P, True)
         group_y(2, HALF, LAST)
-        group_y(2, LAST, BANK)
+        quantize_y(2, 0, HALF)
+        store_codes(2, 0, HALF)
         store_rows(2, HALF, True)
+        group_y(2, LAST, BANK)
         quantize_y(2, HALF, LAST)
         quantize_y(2, LAST, BANK)
         store_rows(2, LAST, True, (nc.scalar,))

@@ -362,11 +362,11 @@ def tile_beam_power_log_bands_h2_kernel(
         y_blocks = kept("y_blocks", [P, 2, PACK, HALF], F32)
         y_rows = kept("y_rows", [P, BANK * PACK], F32)
 
-        def affine_halves(slots):
+        def affine_halves(slots, h0=0, h1=2):
             for u in slots:
                 nc.vector.tensor_scalar(
-                    out=y_halves[:, :, u, :],
-                    in0=logs[0][:, u, :].rearrange("p (h m) -> p h m", h=2),
+                    out=y_halves[:, h0:h1, u, :],
+                    in0=logs[0][:, u, HALF * h0 : HALF * h1].rearrange("p (h m) -> p h m", m=HALF),
                     scalar1=gamma_col[:, u : u + 1],
                     scalar2=beta_col[:, u : u + 1],
                     op0=ALU.mult,
@@ -485,7 +485,7 @@ def tile_beam_power_log_bands_h2_kernel(
         quantize_h(0, 0)
         quantize_h(0, 1)
 
-        SHARE = 192
+        SHARE = 160
         narrow_beams(1, 0, 0, HALF)
         power(1, 0, 0, HALF)
         narrow_beams(1, 0, HALF, BANK)
@@ -494,7 +494,9 @@ def tile_beam_power_log_bands_h2_kernel(
             bands(0, (u,))
         affine_halves((0,))
         quantize_h(1, 0)
-        affine_halves((1, 2, 3))
+        affine_halves((1, 2))
+        affine_halves((3,), 0, 1)
+        affine_halves((3,), 1, 2)
         beams(1, 8, 16)
         group_half(0, 0, SHARE, True)
         turn_blocks(0)
@@ -506,60 +508,64 @@ def tile_beam_power_log_bands_h2_kernel(
         join_half(1, P, HALF)
         store_blocks((0, 1), nc.sync)
         quantize_h(1, 1)
-        beams(2, 0, 6)
+        beams(2, 0, 7)
         store_blocks((2, 3), nc.scalar)
-        beams(2, 6, 8)
+        beams(2, 7, 8)
         group_half(0, SHARE, HALF)
         group_half(1, 0, HALF)
-        narrow_beams(2, 1, 0, HALF, (0,))
+        narrow_beams(2, 1, 0, HALF, (0, 1))
         for u in range(PACK):
             bands(1, (u,))
         quantize_y(0)
         store_codes(0)
         store_scales(0, BANK)
         power(2, 0)
-        affine(1, (0, 1, 2, 3))
+        affine(1)
         quantize_h(2, 0)
-        narrow_beams(2, 1, 0, HALF, (1, 2, 3))
-        narrow_beams(2, 1, HALF, LAST)
-        group_y(1, 0, HALF)
+        narrow_beams(2, 1, 0, HALF, (2, 3))
+        group_y(1, 0, P)
         power(2, 1, 0, HALF)
-        turn(1, 0, HALF)
-        narrow_beams(2, 1, LAST, BANK)
-        store_rows(1, 0, False)
-        quantize_h(2, 1, 0, HALF)
-        power(2, 1, HALF, LAST)
-        turn(1, HALF, BANK)
-        store_rows(1, P, False)
+        narrow_beams(2, 1, HALF, LAST, (0, 1))
+        turn(1, 0, LAST)
+        store_rows(1, 0, True)
+        store_rows(1, P, True)
         store_rows(1, HALF, True)
-        store_rows(1, LAST, True)
-        quantize_h(2, 1, HALF, LAST)
+        narrow_beams(2, 1, HALF, LAST, (2, 3))
+        group_y(1, P, HALF)
+        quantize_h(2, 1, 0, HALF)
+        group_y(1, HALF, BANK)
+        narrow_beams(2, 1, LAST, BANK, (0, 1))
         bands(2, (0, 1), 0, HALF)
+        narrow_beams(2, 1, LAST, BANK, (2, 3))
         bands(2, (2, 3), 0, HALF)
+        power(2, 1, HALF, LAST)
+        quantize_y(1)
+        store_codes(1)
+        quantize_h(2, 1, HALF, LAST)
+        affine(2, (0, 1), 0, HALF)
         power(2, 1, LAST, BANK)
-        group_y(1, HALF, LAST)
+        affine(2, (2, 3), 0, HALF)
         quantize_h(2, 1, LAST, BANK)
+        turn(1, LAST, BANK)
+        store_rows(1, LAST, True)
         bands_open(2, ALL, HALF, LAST)
         bands_close(2, ALL, HALF, LAST)
         bands_open(2, ALL, LAST, BANK)
-        bands_close(2, ALL, LAST, BANK)
-        group_y(1, LAST, BANK)
-        affine(2, ALL, 0, HALF)
-        turn(2, 0, HALF)
-        quantize_y(1)
-        store_codes(1)
-        affine(2, ALL, HALF, LAST)
+        turn(2, 0, P)
         store_rows(2, 0, True)
-        group_y(2, 0, P)
-        affine(2, ALL, LAST, BANK)
-        turn(2, HALF, BANK)
-        group_y(2, P, HALF)
-        store_rows(2, P, True)
-        group_y(2, HALF, LAST)
+        bands_close(2, ALL, LAST, BANK)
+        turn(2, P, HALF)
+        group_y(2, 0, HALF)
+        affine(2, ALL, HALF, LAST)
+        turn(2, HALF, LAST)
         quantize_y(2, 0, HALF)
         store_codes(2, 0, HALF)
-        store_rows(2, HALF, True)
+        affine(2, ALL, LAST, BANK)
+        turn(2, LAST, BANK)
+        store_rows(2, P, True)
+        group_y(2, HALF, LAST)
         group_y(2, LAST, BANK)
+        store_rows(2, HALF, True)
         quantize_y(2, HALF, LAST)
         quantize_y(2, LAST, BANK)
         store_rows(2, LAST, True, (nc.scalar,))

@@ -44,17 +44,17 @@ def tile_beam_power_log_bands_h2_kernel(
         ws_im = kept("ws_im", [P, 2, F], U8)
         xs_first = kept("xs_first", [P, 2, BANK], U8)
         xs_rest = kept("xs_rest", [P, 2, 2 * BANK], U8)
-        one = kept("one", [P, 1], F32)
         warm_root = kept("warm_root", [P, 1], F32)
         warm_ln = kept("warm_ln", [P, 1], F32)
         warm_bf = kept("warm_bf", [P, PACK * P], BF16)
-        warm_codes = kept("warm_codes", [P, P], U32)
-        warm_plane = kept("warm_plane", [P, P], U8)
+        warm_codes = kept("warm_codes", [P, BANK], U32)
+        warm_plane = kept("warm_plane", [P, BANK], U8)
         ident = kept("ident", [P, P], F32)
         base_col = kept("base_col", [P, PACK], BF16)
         gamma_col = kept("gamma_col", [P, PACK], BF16)
         beta_col = kept("beta_col", [P, PACK], BF16)
-        cal_rows = kept("cal_rows", [P, 2 * P], BF16)
+        cal_tile = kept("cal_tile", [P, 2 * P + 16], BF16)
+        cal_rows = cal_tile[:, 0 : 2 * P]
         inv_root = kept("inv_root", [P, 2 * P], F32)
         root_rows = [kept("root_rows%d" % g, [P, P], F32) for g in range(2)]
         roots = kept("roots", [P, 2 * PACK, 32], F32)
@@ -411,12 +411,12 @@ def tile_beam_power_log_bands_h2_kernel(
                 )
 
         def warm_tensor(passes, moving):
-            idle = new_bank([P, P])
+            idle = new_bank([P, BANK])
             for i in range(passes):
                 nc.tensor.matmul_mx(
                     out=idle[:],
-                    lhsT=warm_codes[:].bitcast(FP8X4),
-                    lhsT_scale=warm_plane[:],
+                    lhsT=warm_codes[:, 0:P].bitcast(FP8X4),
+                    lhsT_scale=warm_plane[:, 0:P],
                     rhs=moving.bitcast(FP8X4),
                     rhs_scale=warm_plane[:],
                     start=True,
@@ -424,22 +424,22 @@ def tile_beam_power_log_bands_h2_kernel(
                 )
 
         load_w(RE0, nc.scalar)
-        nc.gpsimd.memset(one[:], 1.0)
-        nc.scalar.activation(out=warm_root[:], in_=one[:], func=ACT.Abs_reciprocal_sqrt, bias=TINY)
-        zero_plane(cal_rows)
+        zero_plane(cal_tile)
+        nc.scalar.activation(out=warm_root[:], in_=cal_tile[:, 2 * P : 2 * P + 1], func=ACT.Abs_reciprocal_sqrt, bias=TINY)
         zero_plane(ws_re)
         zero_plane(xs_first)
         nc.vector.memset(warm_bf[:].bitcast(F32), 1.0)
-        zero_plane(ws_im)
-        nc.vector.quantize_mx(out=warm_codes[:].bitcast(FP8X4), scales=warm_plane[:], in_=warm_bf[:])
-        zero_plane(xs_rest)
+        nc.vector.memset(warm_plane[:, P:BANK].bitcast(I32), 0)
+        nc.vector.memset(warm_codes[:, P:BANK], 0)
+        nc.vector.quantize_mx(out=warm_codes[:, 0:P].bitcast(FP8X4), scales=warm_plane[:, 0:P], in_=warm_bf[:])
         nc.vector.memset(ident[:], 0.0)
+        zero_plane(ws_im)
         make_identity(nc, ident[:], nomemset=True)
         load_cal(nc.sync)
         load_scales(ws_re, w_scales, 0, F)
         load_x(0)
         inverse_root_of_cal()
-        nc.scalar.activation(out=warm_ln[:], in_=one[:], func=ACT.Ln)
+        nc.scalar.activation(out=warm_ln[:], in_=warm_bf[:, 0:2].bitcast(F32), func=ACT.Ln)
         load_scales(xs_first, x_scales, 0, BANK)
         load_w(RE1)
         load_pool(0)
@@ -447,13 +447,7 @@ def tile_beam_power_log_bands_h2_kernel(
         load_w(IM0)
         load_pool(1)
         load_w(IM1)
-        load_scales(xs_rest, x_scales, BANK, M)
-        load_x(1)
-        load_band_column(base_col, base)
-        load_band_column(gamma_col, gamma)
-        load_band_column(beta_col, beta)
-        load_x(2)
-        warm_tensor(16, warm_codes[:])
+        warm_tensor(4, warm_codes[:])
         order_w_codes(RE0)
         order_w_planes(RE0)
         root_of_cal(0)
@@ -461,7 +455,14 @@ def tile_beam_power_log_bands_h2_kernel(
         turn_root(0)
         turn_root(1)
         order_w_planes(RE1)
+        zero_plane(xs_rest)
         sign_of_cal()
+        load_scales(xs_rest, x_scales, BANK, M)
+        load_x(1)
+        load_band_column(base_col, base)
+        load_band_column(gamma_col, gamma)
+        load_band_column(beta_col, beta)
+        load_x(2)
 
         beams(0, 0, 4)
         order_w_codes(RE1)

from contextlib import ExitStack

import concourse.mybir as mybir
from concourse.masks import make_identity

M, K, F, D, N = 1536, 1024, 1024, 2048, 512
FLOPS = 2 * M * K * D + 2 * M * F * N

F32 = mybir.dt.float32
BF16 = mybir.dt.bfloat16
I32 = mybir.dt.int32
U32 = mybir.dt.uint32
U8 = mybir.dt.uint8
FP8X4 = mybir.dt.float8_e4m3fn_x4
FP4X4 = mybir.dt.float4_e2m1fn_x4
ACT = mybir.ActivationFunctionType
ALU = mybir.AluOpType

P = 128
PACK = 4
BANK = 512
RE0, RE1, IM0, IM1 = 0, 1, 2, 3
TINY = 1e-26
CHUNKS = ((0, 512), (512, 512), (1024, 512))


def tile_beam_power_log_bands_h2_kernel(
    tc, x_words, x_scales, w_words, w_scales, cal, pool, base, gamma, beta, out_0, out_1, out_2
):
    nc = tc.nc
    with ExitStack() as ctx:
        keep = ctx.enter_context(tc.tile_pool(name="keep", bufs=1))
        work = ctx.enter_context(tc.tile_pool(name="work", bufs=2))
        psum = ctx.enter_context(tc.psum_pool(name="psum", bufs=8))
        ctx.enter_context(tc.manual_schedule())

        def kept(name, shape, dtype):
            return keep.tile(shape, dtype, name=name, align_bytes=256)

        def new_bank(shape):
            return psum.tile(shape, F32, name="bank", tag="bank")

        ws_re = kept("ws_re", [P, 2, F], U8)
        ws_im = kept("ws_im", [P, 2, F], U8)
        xs_first = kept("xs_first", [P, 2, BANK], U8)
        xs_rest = kept("xs_rest", [P, 2, 2 * BANK], U8)
        warm_root = kept("warm_root", [P, 1], F32)
        warm_ln = kept("warm_ln", [P, 1], F32)
        warm_bf = kept("warm_bf", [P, PACK * P], BF16)
        warm_codes = kept("warm_codes", [P, BANK], U32)
        warm_plane = kept("warm_plane", [P, BANK], U8)
        ident = kept("ident", [P, P], F32)
        base_col = kept("base_col", [P, PACK], BF16)
        gamma_col = kept("gamma_col", [P, PACK], BF16)
        beta_col = kept("beta_col", [P, PACK], BF16)
        cal_tile = kept("cal_tile", [P, 2 * P + 16], BF16)
        cal_rows = cal_tile[:, 0 : 2 * P]
        inv_root = kept("inv_root", [P, 2 * P], F32)
        root_rows = [kept("root_rows%d" % g, [P, P], F32) for g in range(2)]
        roots = kept("roots", [P, 2 * PACK, 32], F32)
        half_sign = kept("half_sign", [P, 2 * PACK], F32)
        w_raw = [kept("w_raw%d" % q, [P, 2, 2 * BANK], U8) for q in range(4)]
        w_codes = [kept("w_codes%d" % q, [P, 2, 2 * BANK], U8) for q in range(4)]
        im_planes = kept("im_planes", [P, 2, F], U8)
        w_planes = [kept("w_planes%d" % q, [P, 2, BANK], U8) for q in (RE0, RE1)]
        w_planes.extend((im_planes[:, :, 0:BANK], im_planes[:, :, BANK:F]))
        x_codes = [kept("x_codes%d" % i, [P, 2, BANK], U32) for i in range(3)]
        pool_raw = [kept("pool_raw%d" % g, [P, PACK, N], BF16) for g in range(2)]
        pool_grouped = [kept("pool_grouped%d" % g, [P, N * PACK], BF16) for g in range(2)]
        pool_codes = [kept("pool_codes%d" % g, [P, N], U32) for g in range(2)]
        pool_planes = [kept("pool_planes%d" % g, [P, N], U8) for g in range(2)]
        y_codes = [kept("y_codes%d" % c, [P, width], U32) for c, (first, width) in enumerate(CHUNKS)]
        y_plane = kept("y_plane", [P, M], U8)

        def zero_plane(plane):
            nc.vector.memset(plane[:].bitcast(I32), 0)

        def load_scales(plane, scales, col0, col1, rows=range(4), queue=nc.sync):
            by_row = scales.rearrange("g (q r) n -> r q g n", r=4)
            for r in rows:
                queue.dma_start(
                    out=plane[r:P:32, :, :].bitcast(I32),
                    in_=by_row[r][:, :, col0:col1].bitcast(I32),
                )

        def load_w(q, queue=nc.sync):
            src = w_words.rearrange("g p b -> p g b")[:, :, 2 * BANK * q : 2 * BANK * (q + 1)]
            queue.dma_start(out=w_raw[q][:].bitcast(I32), in_=src.bitcast(I32))

        def load_x(i, kps=slice(0, 2), queue=nc.sync):
            src = x_words.rearrange("g p m t -> p g (m t)")[:, kps, PACK * BANK * i : PACK * BANK * (i + 1)]
            queue.dma_start(out=x_codes[i][:, kps, :].bitcast(I32), in_=src.bitcast(I32))

        def load_pool(g):
            by_slot = pool.rearrange("(g b t r) n -> g t b r n", g=2, t=PACK, r=8)
            for t in range(PACK):
                nc.sync.dma_start(out=pool_raw[g][:, t, :], in_=by_slot[g][t])

        def load_cal(queue):
            queue.dma_start(
                out=cal_rows[0:P:32, :].rearrange("q (g c) -> q g c", g=2),
                in_=cal.rearrange("(g q c) -> q g c", g=2, q=4),
            )

        def load_band_column(col, vec):
            nc.sync.dma_start(out=col[:], in_=vec.rearrange("(p t) -> p t", t=PACK))

        def inverse_root_of_cal():
            nc.scalar.activation(out=inv_root[:], in_=cal_rows[:], func=ACT.Abs_reciprocal_sqrt, bias=TINY)

        def root_of_cal(g):
            cols = slice(P * g, P * (g + 1))
            nc.vector.tensor_tensor(
                out=root_rows[g][:].rearrange("p (t b r) -> p t b r", t=PACK, r=8),
                in0=inv_root[:, cols].rearrange("p (b t r) -> p t b r", t=PACK, r=8),
                in1=cal_rows[:, cols].rearrange("p (b t r) -> p t b r", t=PACK, r=8),
                op=ALU.mult,
            )

        def turn_root(g):
            nc.vector.transpose(
                out=roots[:, PACK * g : PACK * (g + 1), :].rearrange("p j c -> p (j c)"), in_=root_rows[g][:]
            )

        def sign_of_cal():
            nc.vector.tensor_scalar(
                out=half_sign[:], in0=roots[:, :, 0], scalar1=0.0, scalar2=0.5, op0=ALU.is_ge, op1=ALU.subtract
            )

        def order_w_planes(q):
            raw_plane = (ws_re, ws_im)[q // 2][:, :, BANK * (q % 2) : BANK * (q % 2 + 1)]
            nc.vector.tensor_copy(
                out=w_planes[q][:].bitcast(I32).rearrange("p g (t b w) -> p g t b w", t=PACK, w=2),
                in_=raw_plane.bitcast(I32).rearrange("p g (b t w) -> p g t b w", t=PACK, w=2),
            )

        def order_im_planes():
            nc.vector.tensor_copy(
                out=im_planes[:].bitcast(I32).rearrange("p g (h t b w) -> p (g h) t b w", h=2, t=PACK, w=2),
                in_=ws_im[:].bitcast(I32).rearrange("p g (h b t w) -> p (g h) t b w", h=2, t=PACK, w=2),
            )

        def order_w_codes(q):
            nc.vector.tensor_copy(
                out=w_codes[q][:].bitcast(I32).rearrange("p g (t b w) -> p g t b w", t=PACK, w=4),
                in_=w_raw[q][:].bitcast(I32).rearrange("p g (b t w) -> p g t b w", t=PACK, w=4),
            )

        def order_w(q):
            order_w_codes(q)
            order_w_planes(q)

        def x_operand(first, width, kp):
            i, m0 = divmod(first, BANK)
            plane = xs_first[:, kp, m0 : m0 + width] if i == 0 else xs_rest[:, kp, first - BANK : first - BANK + width]
            return x_codes[i][:, kp, m0 : m0 + width].bitcast(FP8X4), plane

        def beam_passes(out, first, width, q, t):
            for kp in range(2):
                codes, plane = x_operand(first, width, kp)
                nc.tensor.matmul_mx(
                    out=out,
                    lhsT=w_codes[q][:, kp, 2 * P * t : 2 * P * (t + 1)].bitcast(FP4X4),
                    lhsT_scale=w_planes[q][:, kp, P * t : P * (t + 1)],
                    rhs=codes,
                    rhs_scale=plane,
                    start=(kp == 0),
                    stop=(kp == 1),
                )

        squares = {}

        def squares_of(c, g):
            if (c, g) not in squares:
                squares[(c, g)] = work.tile(
                    [P, 2, PACK, CHUNKS[c][1]], F32, name="squares", tag="squares", bufs=3, align_bytes=256
                )
            return squares[(c, g)]

        def span(c, m0, m1):
            return m0, (CHUNKS[c][1] if m1 is None else m1)

        def beam(c, g, t, parts, m0, m1):
            bank = new_bank([P, len(parts), m1 - m0])
            for i, part in enumerate(parts):
                beam_passes(bank[:, i, :], CHUNKS[c][0] + m0, m1 - m0, 2 * part + g, t)
            nc.scalar.activation(
                out=squares_of(c, g)[:, parts[0] : parts[-1] + 1, t, m0:m1],
                in_=bank[:],
                func=ACT.Square,
                scale=roots[:, PACK * g + t, 0:1],
            )

        def beams(c, j0, j1):
            for j in range(j0, j1):
                beam(c, j // 8, j % 4, ((j // 4) % 2,), 0, BANK)

        def narrow_beams(c, g, m0, m1, slots=range(PACK)):
            for t in slots:
                beam(c, g, t, (0, 1), m0, m1)

        h_bf, h_codes, h_planes = {}, {}, {}

        def power(c, g, m0=0, m1=None):
            m0, m1 = span(c, m0, m1)
            if m0 == 0:
                h_bf[(c, g)] = work.tile(
                    [P, CHUNKS[c][1] * PACK], BF16, name="h_bf", tag="h_bf", bufs=2, align_bytes=256
                )
            nc.vector.tensor_tensor(
                out=h_bf[(c, g)][:, PACK * m0 : PACK * m1].rearrange("p (c i t) -> p c t i", i=4, t=PACK),
                in0=squares[(c, g)][:, 0, :, m0:m1].rearrange("p t (c i) -> p c t i", i=4),
                in1=squares[(c, g)][:, 1, :, m0:m1].rearrange("p t (c i) -> p c t i", i=4),
                op=ALU.add,
            )

        def quantize_h(c, g, m0=0, m1=None):
            m0, m1 = span(c, m0, m1)
            if m0 == 0:
                width = CHUNKS[c][1]
                h_codes[(c, g)] = work.tile([P, width], U32, name="h_codes", tag="h_codes", bufs=4, align_bytes=256)
                h_planes[(c, g)] = work.tile([P, width], U8, name="h_plane", tag="h_plane", bufs=4, align_bytes=256)
            nc.vector.quantize_mx(
                out=h_codes[(c, g)][:, m0:m1].bitcast(FP8X4),
                scales=h_planes[(c, g)][:, m0:m1],
                in_=h_bf[(c, g)][:, PACK * m0 : PACK * m1],
            )

        def sign_pool(g):
            for t in range(PACK):
                nc.vector.tensor_scalar(
                    out=pool_raw[g][:, t, :],
                    in0=pool_raw[g][:, t, :],
                    scalar1=half_sign[:, PACK * g + t : PACK * g + t + 1],
                    scalar2=2.0,
                    op0=ALU.mult,
                    op1=ALU.mult,
                )

        def group_pool(g, u0, u1):
            nc.vector.tensor_copy(
                out=pool_grouped[g][:].rearrange("p (u c i t) -> p c t i u", u=PACK, i=2, t=PACK)[:, :, :, :, u0:u1],
                in_=pool_raw[g][:].rearrange("p t (c i u) -> p c t i u", i=2, u=PACK)[:, :, :, :, u0:u1],
            )

        def quantize_pool(g, u0=0, u1=PACK):
            nc.vector.quantize_mx(
                out=pool_codes[g][:, P * u0 : P * u1].bitcast(FP8X4),
                scales=pool_planes[g][:, P * u0 : P * u1],
                in_=pool_grouped[g][:, N * u0 : N * u1],
            )

        logs, ys, y_bf, energy = {}, {}, {}, {}

        def band_pass(out, c, g, u, m0, m1, start, stop):
            nc.tensor.matmul_mx(
                out=out,
                lhsT=pool_codes[g][:, P * u : P * (u + 1)].bitcast(FP8X4),
                lhsT_scale=pool_planes[g][:, P * u : P * (u + 1)],
                rhs=h_codes[(c, g)][:, m0:m1].bitcast(FP8X4),
                rhs_scale=h_planes[(c, g)][:, m0:m1],
                start=start,
                stop=stop,
            )

        def take_log(c, u, m0, m1, src):
            if c not in logs:
                logs[c] = work.tile([P, PACK, CHUNKS[c][1]], F32, name="logs", tag="logs", bufs=2, align_bytes=256)
            nc.scalar.activation(out=logs[c][:, u, m0:m1], in_=src, func=ACT.Ln, bias=base_col[:, u : u + 1])

        def bands(c, slots, m0=0, m1=None):
            m0, m1 = span(c, m0, m1)
            bank = new_bank([P, len(slots), m1 - m0])
            for i, u in enumerate(slots):
                for g in range(2):
                    band_pass(bank[:, i, :], c, g, u, m0, m1, g == 0, g == 1)
            for i, u in enumerate(slots):
                take_log(c, u, m0, m1, bank[:, i, :])

        def bands_open(c, slots, m0, m1):
            energy[(c, slots, m0)] = new_bank([P, len(slots), m1 - m0])
            for i, u in enumerate(slots):
                band_pass(energy[(c, slots, m0)][:, i, :], c, 0, u, m0, m1, i == 0, False)

        def bands_close(c, slots, m0, m1):
            for i, u in enumerate(slots):
                band_pass(energy[(c, slots, m0)][:, i, :], c, 1, u, m0, m1, False, i == len(slots) - 1)
            for i, u in enumerate(slots):
                take_log(c, u, m0, m1, energy[(c, slots, m0)][:, i, :])

        def affine(c, slots=range(PACK), m0=0, m1=None):
            m0, m1 = span(c, m0, m1)
            if c not in ys:
                ys[c] = work.tile([P, PACK, CHUNKS[c][1]], F32, name="ys", tag="ys", bufs=2, align_bytes=256)
            for u in slots:
                nc.vector.tensor_scalar(
                    out=ys[c][:, u, m0:m1],
                    in0=logs[c][:, u, m0:m1],
                    scalar1=gamma_col[:, u : u + 1],
                    scalar2=beta_col[:, u : u + 1],
                    op0=ALU.mult,
                    op1=ALU.add,
                )

        def group_y(c, m0=0, m1=None):
            m0, m1 = span(c, m0, m1)
            if m0 == 0:
                y_bf[c] = work.tile([P, CHUNKS[c][1] * PACK], BF16, name="y_bf", tag="y_bf", bufs=2, align_bytes=256)
            nc.vector.tensor_copy(
                out=y_bf[c][:, PACK * m0 : PACK * m1].rearrange("p (c i u) -> p c u i", i=4, u=PACK),
                in_=ys[c][:, :, m0:m1].rearrange("p u (c i) -> p c u i", i=4),
            )

        def quantize_y(c, m0=0, m1=None):
            m0, m1 = span(c, m0, m1)
            first = CHUNKS[c][0]
            nc.vector.quantize_mx(
                out=y_codes[c][:, m0:m1].bitcast(FP8X4),
                scales=y_plane[:, first + m0 : first + m1],
                in_=y_bf[c][:, PACK * m0 : PACK * m1],
            )

        def store_codes(c, m0=0, m1=BANK):
            first = CHUNKS[c][0]
            dst = out_1[0].rearrange("p m t -> p (m t)")[:, PACK * (first + m0) : PACK * (first + m1)]
            nc.sync.dma_start(out=dst.bitcast(I32), in_=y_codes[c][:, m0:m1].bitcast(I32))

        def store_scales(col0, col1, queues=(nc.sync,) * 4):
            for quad in range(4):
                queues[quad].dma_start(
                    out=out_2[0][4 * quad : 4 * quad + 4, col0:col1].bitcast(I32),
                    in_=y_plane[32 * quad : 32 * quad + 4, col0:col1].bitcast(I32),
                )

        turned = {}

        def turn(c, m0=0, m1=None):
            m0, m1 = span(c, m0, m1)
            for row0 in range(m0, m1, P):
                turned[(c, row0)] = new_bank([P, PACK, P])
                for u in range(PACK):
                    nc.tensor.transpose(turned[(c, row0)][:, u, :], ys[c][:, u, row0 : row0 + P], ident[:])

        def store_rows(c, row0, on_scalar, queues=(nc.sync,)):
            rows = work.tile([P, N], F32, name="rows", tag="rows", bufs=8, align_bytes=256)
            first = CHUNKS[c][0] + row0
            share = P // len(queues)
            for i, queue in enumerate(queues):
                cols = slice(PACK * share * i, PACK * share * (i + 1))
                dst = rows[:, cols].rearrange("m (p u) -> m p u", u=PACK)
                src = turned[(c, row0)][:, :, share * i : share * (i + 1)].rearrange("m u p -> m p u")
                if on_scalar:
                    nc.scalar.copy(out=dst, in_=src)
                else:
                    nc.vector.tensor_copy(out=dst, in_=src)
                queue.dma_start(out=out_0[first : first + P, cols], in_=rows[:, cols])

        HALF = 2 * P
        LAST = 3 * P
        ALL = tuple(range(PACK))
        y_halves = kept("y_halves", [P, 2, PACK, HALF], F32)
        y_blocks = kept("y_blocks", [P, 2, PACK, HALF], F32)
        y_rows = kept("y_rows", [P, BANK * PACK], F32)

        def affine_halves(slots, h0=0, h1=2):
            for u in slots:
                nc.vector.tensor_scalar(
                    out=y_halves[:, h0:h1, u, :],
                    in0=logs[0][:, u, HALF * h0 : HALF * h1].rearrange("p (h m) -> p h m", m=HALF),
                    scalar1=gamma_col[:, u : u + 1],
                    scalar2=beta_col[:, u : u + 1],
                    op0=ALU.mult,
                    op1=ALU.add,
                )

        def turn_blocks(h):
            nc.vector.transpose(
                out=y_blocks[:, h].rearrange("p u m -> p (u m)"), in_=y_halves[:, h].rearrange("p u m -> p (u m)")
            )

        def interleave(dst, src, h, m0, m1, run):
            cols = slice(PACK * (HALF * h + m0), PACK * (HALF * h + m1))
            if run is None:
                nc.gpsimd.tensor_scalar(
                    out=dst[:, cols].rearrange("p (m u) -> p m u", u=PACK),
                    in0=src[:, h, :, m0:m1].rearrange("p u m -> p m u"),
                    scalar1=1.0,
                    scalar2=-0.0,
                    op0=ALU.mult,
                    op1=ALU.add,
                )
            else:
                nc.vector.tensor_copy(
                    out=dst[:, cols].rearrange("p (c i u) -> p c u i", i=run, u=PACK),
                    in_=src[:, h, :, m0:m1].rearrange("p u (c i) -> p c u i", i=run),
                )

        def group_half(h, m0, m1, on_gpsimd=False):
            if 0 not in y_bf:
                y_bf[0] = work.tile([P, BANK * PACK], BF16, name="y_bf", tag="y_bf", bufs=2, align_bytes=256)
            interleave(y_bf[0], y_halves, h, m0, m1, None if on_gpsimd else 4)

        def join_half(h, m0, m1, on_gpsimd=False):
            interleave(y_rows, y_blocks, h, m0, m1, None if on_gpsimd else 2)

        def store_blocks(quads, queue):
            for quad in quads:
                queue.dma_start(
                    out=out_0[0:BANK, P * quad : P * (quad + 1)].rearrange("(j i) n -> i j n", i=32),
                    in_=y_rows[32 * quad : 32 * (quad + 1), :].rearrange("i (j n) -> i j n", n=P),
                )

        def warm_tensor(passes, moving):
            idle = new_bank([P, BANK])
            for i in range(passes):
                nc.tensor.matmul_mx(
                    out=idle[:],
                    lhsT=warm_codes[:, 0:P].bitcast(FP8X4),
                    lhsT_scale=warm_plane[:, 0:P],
                    rhs=moving.bitcast(FP8X4),
                    rhs_scale=warm_plane[:],
                    start=True,
                    stop=True,
                )

        load_w(RE0, nc.scalar)
        zero_plane(cal_tile)
        nc.scalar.activation(out=warm_root[:], in_=cal_tile[:, 2 * P : 2 * P + 1], func=ACT.Abs_reciprocal_sqrt, bias=TINY)
        zero_plane(ws_re)
        zero_plane(xs_first)
        nc.vector.memset(warm_bf[:].bitcast(F32), 1.0)
        nc.vector.memset(warm_plane[:, P:BANK].bitcast(I32), 0)
        nc.vector.memset(warm_codes[:, P:BANK], 0)
        nc.vector.quantize_mx(out=warm_codes[:, 0:P].bitcast(FP8X4), scales=warm_plane[:, 0:P], in_=warm_bf[:])
        nc.vector.memset(ident[:], 0.0)
        zero_plane(ws_im)
        make_identity(nc, ident[:], nomemset=True)
        load_cal(nc.sync)
        load_scales(ws_re, w_scales, 0, F)
        load_x(0)
        inverse_root_of_cal()
        nc.scalar.activation(out=warm_ln[:], in_=warm_bf[:, 0:2].bitcast(F32), func=ACT.Ln)
        load_scales(xs_first, x_scales, 0, BANK)
        load_w(RE1)
        load_pool(0)
        load_scales(ws_im, w_scales, F, D)
        load_w(IM0)
        load_pool(1)
        load_w(IM1)
        warm_tensor(4, warm_codes[:])
        order_w_codes(RE0)
        order_w_planes(RE0)
        root_of_cal(0)
        root_of_cal(1)
        turn_root(0)
        turn_root(1)
        order_w_planes(RE1)
        zero_plane(xs_rest)
        sign_of_cal()
        load_scales(xs_rest, x_scales, BANK, M)
        load_x(1)
        load_band_column(base_col, base)
        load_band_column(gamma_col, gamma)
        load_band_column(beta_col, beta)
        load_x(2)

        beams(0, 0, 4)
        order_w_codes(RE1)
        beams(0, 8, 12)
        sign_pool(0)
        group_pool(0, 0, 2)
        order_im_planes()
        order_w_codes(IM0)
        beams(0, 4, 8)
        group_pool(0, 2, 4)
        sign_pool(1)
        quantize_pool(0)
        order_w_codes(IM1)
        beams(0, 12, 16)
        group_pool(1, 0, 2)
        group_pool(1, 2, 4)
        quantize_pool(1, 0, 2)
        quantize_pool(1, 2, 4)
        power(0, 0)
        power(0, 1)
        quantize_h(0, 0)
        quantize_h(0, 1)

        SHARE = 160
        narrow_beams(1, 0, 0, HALF)
        power(1, 0, 0, HALF)
        narrow_beams(1, 0, HALF, BANK)
        power(1, 0, HALF, BANK)
        for u in range(PACK):
            bands(0, (u,))
        affine_halves((0,))
        quantize_h(1, 0)
        affine_halves((1, 2))
        affine_halves((3,), 0, 1)
        affine_halves((3,), 1, 2)
        beams(1, 8, 16)
        group_half(0, 0, SHARE, True)
        turn_blocks(0)
        join_half(0, 0, SHARE, True)
        turn_blocks(1)
        join_half(0, SHARE, HALF)
        join_half(1, 0, P)
        power(1, 1)
        join_half(1, P, HALF)
        store_blocks((0, 1), nc.sync)
        quantize_h(1, 1)
        beams(2, 0, 7)
        store_blocks((2, 3), nc.scalar)
        beams(2, 7, 8)
        group_half(0, SHARE, HALF)
        group_half(1, 0, HALF)
        narrow_beams(2, 1, 0, HALF, (0, 1))
        for u in range(PACK):
            bands(1, (u,))
        quantize_y(0)
        store_codes(0)
        store_scales(0, BANK)
        power(2, 0)
        affine(1)
        quantize_h(2, 0)
        narrow_beams(2, 1, 0, HALF, (2, 3))
        group_y(1, 0, P)
        power(2, 1, 0, HALF)
        narrow_beams(2, 1, HALF, LAST, (0, 1))
        turn(1, 0, LAST)
        store_rows(1, 0, True)
        store_rows(1, P, True)
        store_rows(1, HALF, True)
        narrow_beams(2, 1, HALF, LAST, (2, 3))
        group_y(1, P, HALF)
        quantize_h(2, 1, 0, HALF)
        group_y(1, HALF, BANK)
        narrow_beams(2, 1, LAST, BANK, (0, 1))
        bands(2, (0, 1), 0, HALF)
        narrow_beams(2, 1, LAST, BANK, (2, 3))
        bands(2, (2, 3), 0, HALF)
        power(2, 1, HALF, LAST)
        quantize_y(1)
        store_codes(1)
        quantize_h(2, 1, HALF, LAST)
        affine(2, (0, 1), 0, HALF)
        power(2, 1, LAST, BANK)
        affine(2, (2, 3), 0, HALF)
        quantize_h(2, 1, LAST, BANK)
        turn(1, LAST, BANK)
        store_rows(1, LAST, True)
        bands_open(2, ALL, HALF, LAST)
        bands_close(2, ALL, HALF, LAST)
        bands_open(2, ALL, LAST, BANK)
        turn(2, 0, P)
        store_rows(2, 0, True)
        bands_close(2, ALL, LAST, BANK)
        turn(2, P, HALF)
        group_y(2, 0, HALF)
        affine(2, ALL, HALF, LAST)
        turn(2, HALF, LAST)
        quantize_y(2, 0, HALF)
        store_codes(2, 0, HALF)
        affine(2, ALL, LAST, BANK)
        turn(2, LAST, BANK)
        store_rows(2, P, True)
        group_y(2, HALF, LAST)
        group_y(2, LAST, BANK)
        store_rows(2, HALF, True)
        quantize_y(2, HALF, LAST)
        quantize_y(2, LAST, BANK)
        store_rows(2, LAST, True, (nc.scalar,))
        store_codes(2, HALF, BANK)
        store_scales(BANK, M)
